import numpy as np
import ml_dtypes


def mxq(x, axis, fmt="e4m3"):
    dtype, down = {"e4m3": (ml_dtypes.float8_e4m3fn, 7), "e5m2": (ml_dtypes.float8_e5m2, 14)}[fmt]
    v = np.moveaxis(np.asarray(x, np.float32).astype(ml_dtypes.bfloat16).astype(np.float64), axis, -1)
    blocks = v.reshape(v.shape[:-1] + (-1, 32))
    amax = np.abs(blocks).max(-1, keepdims=True)
    byte = np.maximum(np.where(amax > 0, np.frexp(amax)[1] - 1 + 127, 0) - down, 1)
    scale = np.exp2(byte - 127.0)
    codes = (blocks / scale).astype(np.float32).astype(dtype).astype(np.float64)
    return np.moveaxis((codes * scale).reshape(v.shape), -1, axis)


WIDE = False


def mx_kscale(k):
    if not WIDE:
        return np.ones(k)
    levels = np.array([10, -10, 5, -5, 0])
    if k % 512:
        return np.exp2(np.random.permutation(np.resize(levels, k // 32))).repeat(32)
    a = np.empty((k // 512, 16))
    for p in range(k // 512):
        a[p, :8] = np.random.permutation(np.resize(levels, 8))
        for g in range(8):
            far = levels[np.abs(levels - a[p, g]) >= 10]
            a[p, g + 8] = far[np.random.randint(len(far))]
    return np.exp2(a.ravel()).repeat(32)


def f64(x):
    return np.asarray(x).astype(np.float64)


def striped(idx):
    return np.tile(idx.reshape(-1, 16).T, (8, 1)).astype(np.uint16)


def unstriped(offs):
    return offs[:16].T.reshape(-1).astype(np.int64)


def pack_weight(w):
    k, n = w.shape
    w = f64(np.asarray(w, np.float32).astype(ml_dtypes.bfloat16)).reshape(k // 32, 32, n)
    amax = np.abs(w).max(1)
    byte = np.clip(np.where(amax > 0, np.frexp(amax)[1] - 1 + 127 - 7, 1), 1, 254)
    scaled = (w * np.exp2(127.0 - byte)[:, None, :]).reshape(k, n).astype(np.float32)
    words = np.ascontiguousarray(scaled.reshape(k // 512, 128, 4, n).transpose(0, 1, 3, 2)).astype(ml_dtypes.float8_e4m3fn).view(np.uint8)
    return words, np.ascontiguousarray(byte.astype(np.uint8).reshape(k // 512, 16, n))


def unpack_weight(words, scales):
    g, p, n, _ = words.shape
    vals = np.ascontiguousarray(words).view(ml_dtypes.float8_e4m3fn).astype(np.float64) * np.repeat(np.exp2(scales.astype(np.float64) - 127.0), 8, axis=1)[..., None]
    return vals.transpose(0, 1, 3, 2).reshape(g * 512, n)


K, T, S, D, N = 1024, 4096, 1024, 8, 128
P = 2 ** 7


def setup_inputs():
    n = np.random.standard_normal
    s = mx_kscale(K)[:, None]
    packed_xT = pack_weight(n((K, T)) * s)
    return {
        "x_words": packed_xT[0],
        "x_scales": packed_xT[1],
        "w1": (n((K, N)) / np.sqrt(K) / s).astype(np.float32),
        "apo": (np.tile(np.random.uniform(0.3, 1.0, S), (P, 1))).astype(np.float32),
        "offs": striped(np.random.permutation(T)[:S]),
    }


def reference(x_words, x_scales, w1, apo, offs):
    xq = unpack_weight(x_words, x_scales)[:, unstriped(offs)]
    y = mxq(f64(w1), 0, "e4m3").T @ xq
    ys = y * f64(apo)[:1]
    beam = ys.reshape(len(ys), -1, D).sum(axis=2)
    y2 = (y) ** 2
    co = ((y.reshape(len(y), -1, D).sum(axis=2)) ** 2) / (8.0 * (y2.reshape(len(y2), -1, D).sum(axis=2)) + 0.1)
    return np.log(np.abs(beam * co) + 0.05)

@@ -1,0 +1,148 @@
+from contextlib import ExitStack
+
+import concourse.mybir as mybir
+from concourse.masks import make_identity
+
+K, T, S, D, M = 1024, 4096, 1024, 8, 128
+P = 128
+PASSES = 2
+V = S // D
+HALF = S // 2
+VH = V // 2
+FLOPS = 2 * K * M * S
+BYTES = K * T + K // 32 * T + K * M * 4 + S * 4 + P * S // 16 * 2 + M * V * 4
+
+F32 = mybir.dt.float32
+BF16 = mybir.dt.bfloat16
+I32 = mybir.dt.int32
+U32 = mybir.dt.uint32
+U16 = mybir.dt.uint16
+U8 = mybir.dt.uint8
+FP8X4 = mybir.dt.float8_e4m3fn_x4
+ALU = mybir.AluOpType
+ACT = mybir.ActivationFunctionType
+AX = mybir.AxisListType
+LN_SHIFT = 2.0 ** -32
+
+
+def tile_picked_ydas_log_p_kernel(tc, x_words, x_scales, w1, apo, offs, out):
+    nc = tc.nc
+    with ExitStack() as ctx:
+        sb = ctx.enter_context(tc.tile_pool(name="sb", bufs=1))
+        ps = ctx.enter_context(tc.psum_pool(name="ps", bufs=1))
+
+        offsets = sb.tile([P, S // 16], U16, name="offsets")
+        apo_vd = sb.tile([P, D], F32, name="apo_vd")
+        nc.scalar.dma_start(apo_vd[:], apo[0:1, :].rearrange("o (v d) -> (o v) d", d=D))
+
+        scale_table = sb.tile([P, T], U8, name="scale_table", tag="scales_then_words", align_bytes=64)
+        nc.vector.memset(scale_table[:].bitcast(I32), 0)
+        nc.scalar.dma_start(
+            scale_table[:].bitcast(I32)[0:P:4, :],
+            x_scales.bitcast(I32).rearrange("o q c -> q o c"),
+        )
+        x_planes = sb.tile([P, PASSES * S], U8, name="x_planes", align_bytes=64)
+        nc.vector.memset(x_planes[:].bitcast(I32), 0)
+
+        w_raw = sb.tile([P, PASSES, 4, M], F32, name="w_raw", tag="w_then_table")
+        nc.sync.dma_start(
+            w_raw[:].rearrange("p o t m -> p o (t m)"),
+            w1.rearrange("(o p t) m -> p o (t m)", o=PASSES, t=4),
+        )
+        nc.sync.dma_start(offsets[:], offs)
+        word_table0 = sb.tile([P, T], I32, name="word_table0")
+        nc.sync.dma_start(word_table0[:], x_words[0].rearrange("p c r -> p (c r)").bitcast(I32))
+
+        w_grouped = sb.tile([P, PASSES, M, 4], BF16, name="w_grouped", align_bytes=64)
+        nc.vector.tensor_copy(w_grouped[:], w_raw[:].rearrange("p o t m -> p o m t"))
+        w_codes = sb.tile([P, PASSES * M], U32, name="w_codes", align_bytes=64)
+        w_plane = sb.tile([P, PASSES * M], U8, name="w_plane", align_bytes=64)
+        nc.vector.quantize_mx(
+            out=w_codes[:].bitcast(FP8X4), scales=w_plane[:], in_=w_grouped[:].rearrange("p o m t -> p (o m t)")
+        )
+        word_table1 = sb.tile([P, T], I32, name="word_table1", tag="w_then_table")
+        nc.sync.dma_start(word_table1[:], x_words[1].rearrange("p c r -> p (c r)").bitcast(I32))
+        word_tables = [word_table0, word_table1]
+
+        ln_warm = sb.tile([P, 1], F32, name="ln_warm")
+        nc.scalar.activation(ln_warm[:], apo_vd[:, 0:1], ACT.Ln, bias=1.0, scale=0.0)
+
+        ident = sb.tile([P, P], F32, name="ident")
+        make_identity(nc, ident[:])
+        apo_dv = sb.tile([P, D, V], F32, name="apo_dv")
+        for g in range(2):
+            apo_ps = ps.tile([P, 4, V], F32, name=f"apo_ps{g}")
+            for i in range(4):
+                d = 4 * g + i
+                nc.tensor.transpose(apo_ps[:, i, :], apo_vd[:, d : d + 1].to_broadcast([P, P]), ident[:])
+            nc.scalar.copy(apo_dv[:, 4 * g : 4 * g + 4, :], apo_ps[:])
+
+        picked_scales = sb.tile([P, S], U8, name="picked_scales")
+        nc.vector.tensor_copy(picked_scales[:], scale_table[:].indirect(offsets[:]))
+        for q in range(4):
+            nc.scalar.dma_start(
+                x_planes[:].bitcast(I32)[32 * q : 32 * q + 4, :],
+                picked_scales[:].bitcast(I32)[32 * q : 32 * q + 32 : 4, :],
+            )
+
+        picked0 = sb.tile([P, S], U32, name="picked0", tag="scales_then_words", align_bytes=64)
+        nc.vector.tensor_copy(picked0[:], word_tables[0][:].bitcast(U32).indirect(offsets[:]))
+
+        def product(bank, o, h, picked):
+            nc.tensor.matmul_mx(
+                out=bank[:],
+                lhsT=w_codes[:, o * M : (o + 1) * M].bitcast(FP8X4),
+                lhsT_scale=w_plane[:, o * M : (o + 1) * M],
+                rhs=picked.bitcast(FP8X4),
+                rhs_scale=x_planes[:, o * S + h * HALF : o * S + (h + 1) * HALF],
+                start=(o == 0),
+                stop=(o == PASSES - 1),
+            )
+
+        y = [ps.tile([P, HALF], F32, name=f"y{h}") for h in range(2)]
+        for h in range(2):
+            product(y[h], 0, h, picked0[:, h * HALF : (h + 1) * HALF])
+        for h in range(2):
+            picked1 = sb.tile([P, HALF], U32, name=f"picked1_{h}", align_bytes=64)
+            cols = slice(h * HALF // 16, (h + 1) * HALF // 16)
+            nc.vector.tensor_copy(picked1[:], word_tables[1][:].bitcast(U32).indirect(offsets[:, cols]))
+            product(y[h], 1, h, picked1[:])
+
+        ys = sb.tile([P, D, V], F32, name="ys")
+        y2 = sb.tile([P, S], F32, name="y2")
+        y_sum = sb.tile([P, V], F32, name="y_sum")
+        y2_sum = sb.tile([P, V], F32, name="y2_sum")
+        for h in range(2):
+            vs = slice(h * VH, (h + 1) * VH)
+            nc.vector.tensor_tensor(
+                ys[:, :, vs], y[h][:].rearrange("p (v d) -> p d v", d=D), apo_dv[:, :, vs], ALU.mult
+            )
+        for h in range(2):
+            nc.scalar.activation(y2[:, h * HALF : (h + 1) * HALF], y[h][:], ACT.Square)
+        for h in range(2):
+            vs = slice(h * VH, (h + 1) * VH)
+            nc.vector.tensor_reduce(y_sum[:, vs], y[h][:].rearrange("p (v d) -> p v d", d=D), AX.X, ALU.add)
+
+        beam_vm = ps.tile([P, M], F32, name="beam_vm")
+        for d in range(D):
+            nc.tensor.matmul(beam_vm[:], ys[:, d, :], ident[:], start=(d == 0), stop=(d == D - 1), is_transpose=True)
+        beam_abs_vm = sb.tile([P, M], F32, name="beam_abs_vm")
+        nc.scalar.activation(beam_abs_vm[:], beam_vm[:], ACT.Abs)
+        beam_abs = ps.tile([P, V], F32, name="beam_abs")
+        nc.tensor.transpose(beam_abs[:], beam_abs_vm[:], ident[:])
+
+        sum_sq = sb.tile([P, V], F32, name="sum_sq")
+        nc.scalar.activation(sum_sq[:], y_sum[:], ACT.Square)
+        nc.vector.tensor_reduce(y2_sum[:], y2[:].rearrange("p (v d) -> p v d", d=D), AX.X, ALU.add)
+
+        ln_den = sb.tile([P, V], F32, name="ln_den")
+        nc.scalar.activation(ln_den[:], y2_sum[:], ACT.Ln, bias=0.1 * LN_SHIFT, scale=8.0 * LN_SHIFT)
+        power = sb.tile([P, V], F32, name="power")
+        nc.vector.tensor_tensor(power[:], beam_abs[:], sum_sq[:], ALU.mult)
+        num = sb.tile([P, V], F32, name="num")
+        nc.vector.scalar_tensor_tensor(num[:], y2_sum[:], 0.4, power[:], ALU.mult, ALU.add)
+        ln_num = sb.tile([P, V], F32, name="ln_num")
+        nc.scalar.activation(ln_num[:], num[:], ACT.Ln, bias=0.005 * LN_SHIFT, scale=LN_SHIFT)
+        result = sb.tile([P, V], F32, name="result")
+        nc.vector.tensor_tensor(result[:], ln_num[:], ln_den[:], ALU.subtract)
+        nc.sync.dma_start(out, result[:])

@@ -69,7 +69,7 @@ def tile_picked_ydas_log_p_kernel(tc, x_words, x_scales, w1, apo, offs, out):
 
         ident = sb.tile([P, P], F32, name="ident")
         make_identity(nc, ident[:])
-        apo_dv = sb.tile([P, D, V], F32, name="apo_dv")
+        apo_dv = sb.tile([P, D, V], F32, name="apo_dv", tag="apo_then_sum")
         for g in range(2):
             apo_ps = ps.tile([P, 4, V], F32, name=f"apo_ps{g}")
             for i in range(4):
@@ -80,7 +80,7 @@ def tile_picked_ydas_log_p_kernel(tc, x_words, x_scales, w1, apo, offs, out):
         picked_scales = sb.tile([P, S], U8, name="picked_scales")
         nc.vector.tensor_copy(picked_scales[:], scale_table[:].indirect(offsets[:]))
         for q in range(4):
-            nc.scalar.dma_start(
+            nc.sync.dma_start(
                 x_planes[:].bitcast(I32)[32 * q : 32 * q + 4, :],
                 picked_scales[:].bitcast(I32)[32 * q : 32 * q + 32 : 4, :],
             )
@@ -101,24 +101,29 @@ def tile_picked_ydas_log_p_kernel(tc, x_words, x_scales, w1, apo, offs, out):
 
         y = [ps.tile([P, HALF], F32, name=f"y{h}") for h in range(2)]
         for h in range(2):
-            product(y[h], 0, h, picked0[:, h * HALF : (h + 1) * HALF])
-        for h in range(2):
             picked1 = sb.tile([P, HALF], U32, name=f"picked1_{h}", align_bytes=64)
             cols = slice(h * HALF // 16, (h + 1) * HALF // 16)
             nc.vector.tensor_copy(picked1[:], word_tables[1][:].bitcast(U32).indirect(offsets[:, cols]))
+            product(y[h], 0, h, picked0[:, h * HALF : (h + 1) * HALF])
             product(y[h], 1, h, picked1[:])
 
         ys = sb.tile([P, D, V], F32, name="ys")
-        y2 = sb.tile([P, S], F32, name="y2")
-        y_sum = sb.tile([P, V], F32, name="y_sum")
+        y2 = [sb.tile([P, HALF], F32, name=f"y2_{h}") for h in range(2)]
         y2_sum = sb.tile([P, V], F32, name="y2_sum")
+        y_dv = [y[h][:].rearrange("p (v d) -> p d v", d=D) for h in range(2)]
         for h in range(2):
             vs = slice(h * VH, (h + 1) * VH)
-            nc.vector.tensor_tensor(
-                ys[:, :, vs], y[h][:].rearrange("p (v d) -> p d v", d=D), apo_dv[:, :, vs], ALU.mult
-            )
-        for h in range(2):
-            nc.scalar.activation(y2[:, h * HALF : (h + 1) * HALF], y[h][:], ACT.Square)
+            nc.vector.tensor_tensor(ys[:, :, vs], y_dv[h], apo_dv[:, :, vs], ALU.mult)
+        nc.scalar.activation(y2[0][:].rearrange("p (d v) -> p d v", d=D), y_dv[0], ACT.Square)
+        nc.scalar.activation(y2[1][:], y[1][:], ACT.Square)
+
+        four = sb.tile([P, 4 * VH], F32, name="four")
+        two = sb.tile([P, 2 * VH], F32, name="two")
+        nc.gpsimd.tensor_tensor(four[:], y2[0][:, : 4 * VH], y2[0][:, 4 * VH :], ALU.add)
+        nc.gpsimd.tensor_tensor(two[:], four[:, : 2 * VH], four[:, 2 * VH :], ALU.add)
+        nc.gpsimd.tensor_tensor(y2_sum[:, :VH], two[:, :VH], two[:, VH:], ALU.add)
+
+        y_sum = sb.tile([P, V], F32, name="y_sum", tag="apo_then_sum")
         for h in range(2):
             vs = slice(h * VH, (h + 1) * VH)
             nc.vector.tensor_reduce(y_sum[:, vs], y[h][:].rearrange("p (v d) -> p v d", d=D), AX.X, ALU.add)
@@ -133,7 +138,7 @@ def tile_picked_ydas_log_p_kernel(tc, x_words, x_scales, w1, apo, offs, out):
 
         sum_sq = sb.tile([P, V], F32, name="sum_sq")
         nc.scalar.activation(sum_sq[:], y_sum[:], ACT.Square)
-        nc.vector.tensor_reduce(y2_sum[:], y2[:].rearrange("p (v d) -> p v d", d=D), AX.X, ALU.add)
+        nc.vector.tensor_reduce(y2_sum[:, VH:], y2[1][:].rearrange("p (v d) -> p v d", d=D), AX.X, ALU.add)
 
         ln_den = sb.tile([P, V], F32, name="ln_den")
         nc.scalar.activation(ln_den[:], y2_sum[:], ACT.Ln, bias=0.1 * LN_SHIFT, scale=8.0 * LN_SHIFT)

@@ -9,6 +9,8 @@ PASSES = 2
 V = S // D
 HALF = S // 2
 VH = V // 2
+QUARTER = S // 4
+VQ = V // 4
 FLOPS = 2 * K * M * S
 BYTES = K * T + K // 32 * T + K * M * 4 + S * 4 + P * S // 16 * 2 + M * V * 4
 
@@ -23,6 +25,7 @@ ALU = mybir.AluOpType
 ACT = mybir.ActivationFunctionType
 AX = mybir.AxisListType
 LN_SHIFT = 2.0 ** -32
+SQ_SCALE = 0.4 ** 0.5
 
 
 def tile_picked_ydas_log_p_kernel(tc, x_words, x_scales, w1, apo, offs, out):
@@ -69,13 +72,15 @@ def tile_picked_ydas_log_p_kernel(tc, x_words, x_scales, w1, apo, offs, out):
 
         ident = sb.tile([P, P], F32, name="ident")
         make_identity(nc, ident[:])
-        apo_dv = sb.tile([P, D, V], F32, name="apo_dv", tag="apo_then_sum")
+        apo_dv = sb.tile([P, D, VH], F32, name="apo_dv")
+        apo_vd2 = sb.tile([P, VH, D], F32, name="apo_vd2")
         for g in range(2):
             apo_ps = ps.tile([P, 4, V], F32, name=f"apo_ps{g}")
             for i in range(4):
                 d = 4 * g + i
                 nc.tensor.transpose(apo_ps[:, i, :], apo_vd[:, d : d + 1].to_broadcast([P, P]), ident[:])
-            nc.scalar.copy(apo_dv[:, 4 * g : 4 * g + 4, :], apo_ps[:])
+            nc.scalar.copy(apo_dv[:, 4 * g : 4 * g + 4, :], apo_ps[:, :, :VH])
+            nc.scalar.copy(apo_vd2[:, :, 4 * g : 4 * g + 4], apo_ps[:, :, VH:].rearrange("p d v -> p v d"))
 
         picked_scales = sb.tile([P, S], U8, name="picked_scales")
         nc.vector.tensor_copy(picked_scales[:], scale_table[:].indirect(offsets[:]))
@@ -88,64 +93,83 @@ def tile_picked_ydas_log_p_kernel(tc, x_words, x_scales, w1, apo, offs, out):
         picked0 = sb.tile([P, S], U32, name="picked0", tag="scales_then_words", align_bytes=64)
         nc.vector.tensor_copy(picked0[:], word_tables[0][:].bitcast(U32).indirect(offsets[:]))
 
-        def product(bank, o, h, picked):
+        def product(bank, o, c, picked):
             nc.tensor.matmul_mx(
                 out=bank[:],
                 lhsT=w_codes[:, o * M : (o + 1) * M].bitcast(FP8X4),
                 lhsT_scale=w_plane[:, o * M : (o + 1) * M],
                 rhs=picked.bitcast(FP8X4),
-                rhs_scale=x_planes[:, o * S + h * HALF : o * S + (h + 1) * HALF],
+                rhs_scale=x_planes[:, o * S + c * QUARTER : o * S + (c + 1) * QUARTER],
                 start=(o == 0),
                 stop=(o == PASSES - 1),
             )
 
-        y = [ps.tile([P, HALF], F32, name=f"y{h}") for h in range(2)]
+        y = [ps.tile([P, QUARTER], F32, name=f"y{c}") for c in range(4)]
         for h in range(2):
             picked1 = sb.tile([P, HALF], U32, name=f"picked1_{h}", align_bytes=64)
             cols = slice(h * HALF // 16, (h + 1) * HALF // 16)
             nc.vector.tensor_copy(picked1[:], word_tables[1][:].bitcast(U32).indirect(offsets[:, cols]))
-            product(y[h], 0, h, picked0[:, h * HALF : (h + 1) * HALF])
-            product(y[h], 1, h, picked1[:])
+            for c in (2 * h, 2 * h + 1):
+                product(y[c], 0, c, picked0[:, c * QUARTER : (c + 1) * QUARTER])
+            for i in range(2):
+                product(y[2 * h + i], 1, 2 * h + i, picked1[:, i * QUARTER : (i + 1) * QUARTER])
 
-        ys = sb.tile([P, D, V], F32, name="ys")
-        y2 = [sb.tile([P, HALF], F32, name=f"y2_{h}") for h in range(2)]
-        y2_sum = sb.tile([P, V], F32, name="y2_sum")
-        y_dv = [y[h][:].rearrange("p (v d) -> p d v", d=D) for h in range(2)]
-        for h in range(2):
-            vs = slice(h * VH, (h + 1) * VH)
-            nc.vector.tensor_tensor(ys[:, :, vs], y_dv[h], apo_dv[:, :, vs], ALU.mult)
-        nc.scalar.activation(y2[0][:].rearrange("p (d v) -> p d v", d=D), y_dv[0], ACT.Square)
-        nc.scalar.activation(y2[1][:], y[1][:], ACT.Square)
-
-        four = sb.tile([P, 4 * VH], F32, name="four")
-        two = sb.tile([P, 2 * VH], F32, name="two")
-        nc.gpsimd.tensor_tensor(four[:], y2[0][:, : 4 * VH], y2[0][:, 4 * VH :], ALU.add)
-        nc.gpsimd.tensor_tensor(two[:], four[:, : 2 * VH], four[:, 2 * VH :], ALU.add)
-        nc.gpsimd.tensor_tensor(y2_sum[:, :VH], two[:, :VH], two[:, VH:], ALU.add)
-
-        y_sum = sb.tile([P, V], F32, name="y_sum", tag="apo_then_sum")
-        for h in range(2):
-            vs = slice(h * VH, (h + 1) * VH)
-            nc.vector.tensor_reduce(y_sum[:, vs], y[h][:].rearrange("p (v d) -> p v d", d=D), AX.X, ALU.add)
-
-        beam_vm = ps.tile([P, M], F32, name="beam_vm")
+        y_dv = [y[c][:].rearrange("p (v d) -> p d v", d=D) for c in range(4)]
+        y_vd = [y[c][:].rearrange("p (v d) -> p v d", d=D) for c in range(4)]
+        stacked = sb.tile([P, D, 2, VH], F32, name="stacked")
+        y_sum = sb.tile([P, V], F32, name="y_sum")
+        for c in range(2):
+            nc.scalar.activation(stacked[:, :, 1, c * VQ : (c + 1) * VQ], y_dv[c], ACT.Square, scale=SQ_SCALE)
+        for c in range(2):
+            vs = slice(c * VQ, (c + 1) * VQ)
+            nc.vector.tensor_tensor(stacked[:, :, 0, vs], y_dv[c], apo_dv[:, :, vs], ALU.mult)
+        sums_t = ps.tile([P, M], F32, name="sums_t")
         for d in range(D):
-            nc.tensor.matmul(beam_vm[:], ys[:, d, :], ident[:], start=(d == 0), stop=(d == D - 1), is_transpose=True)
-        beam_abs_vm = sb.tile([P, M], F32, name="beam_abs_vm")
-        nc.scalar.activation(beam_abs_vm[:], beam_vm[:], ACT.Abs)
-        beam_abs = ps.tile([P, V], F32, name="beam_abs")
-        nc.tensor.transpose(beam_abs[:], beam_abs_vm[:], ident[:])
+            nc.tensor.matmul(
+                sums_t[:],
+                stacked[:, d].rearrange("p s v -> p (s v)"),
+                ident[:],
+                start=(d == 0),
+                stop=(d == D - 1),
+                is_transpose=True,
+            )
+        for c in range(2):
+            nc.vector.tensor_reduce(y_sum[:, c * VQ : (c + 1) * VQ], y_vd[c], AX.X, ALU.add)
+
+        sq = sb.tile([P, VH, D], F32, name="sq")
+        ys = sb.tile([P, VH, D], F32, name="ys")
+        for c in range(2):
+            nc.scalar.activation(sq[:, c * VQ : (c + 1) * VQ, :], y_vd[2 + c], ACT.Square, scale=SQ_SCALE)
+        for c in range(2):
+            vs = slice(c * VQ, (c + 1) * VQ)
+            nc.vector.tensor_tensor(ys[:, vs, :], y_vd[2 + c], apo_vd2[:, vs, :], ALU.mult)
+        for c in range(2):
+            nc.vector.tensor_reduce(y_sum[:, VH + c * VQ : VH + (c + 1) * VQ], y_vd[2 + c], AX.X, ALU.add)
+        beam2 = sb.tile([P, VH], F32, name="beam2")
+        nc.vector.tensor_reduce(beam2[:], ys[:], AX.X, ALU.add)
+
+        energy2 = sb.tile([P, VH], F32, name="energy2")
+        nc.vector.tensor_reduce(energy2[:], sq[:], AX.X, ALU.add)
+
+        abs_t = sb.tile([P, M], F32, name="abs_t")
+        nc.scalar.activation(abs_t[:], sums_t[:], ACT.Abs)
+        sums1 = ps.tile([P, 2, VH], F32, name="sums1")
+        nc.tensor.transpose(sums1[:].rearrange("p s v -> p (s v)"), abs_t[:], ident[:])
 
         sum_sq = sb.tile([P, V], F32, name="sum_sq")
         nc.scalar.activation(sum_sq[:], y_sum[:], ACT.Square)
-        nc.vector.tensor_reduce(y2_sum[:, VH:], y2[1][:].rearrange("p (v d) -> p v d", d=D), AX.X, ALU.add)
-
+        beam2_abs = sb.tile([P, VH], F32, name="beam2_abs")
+        nc.scalar.activation(beam2_abs[:], beam2[:], ACT.Abs)
         ln_den = sb.tile([P, V], F32, name="ln_den")
-        nc.scalar.activation(ln_den[:], y2_sum[:], ACT.Ln, bias=0.1 * LN_SHIFT, scale=8.0 * LN_SHIFT)
+        nc.scalar.activation(ln_den[:, VH:], energy2[:], ACT.Ln, bias=0.1 * LN_SHIFT, scale=20.0 * LN_SHIFT)
+
         power = sb.tile([P, V], F32, name="power")
-        nc.vector.tensor_tensor(power[:], beam_abs[:], sum_sq[:], ALU.mult)
         num = sb.tile([P, V], F32, name="num")
-        nc.vector.scalar_tensor_tensor(num[:], y2_sum[:], 0.4, power[:], ALU.mult, ALU.add)
+        nc.vector.tensor_tensor(power[:, :VH], sums1[:, 0, :], sum_sq[:, :VH], ALU.mult)
+        nc.vector.tensor_tensor(power[:, VH:], beam2_abs[:], sum_sq[:, VH:], ALU.mult)
+        nc.vector.tensor_tensor(num[:, :VH], sums1[:, 1, :], power[:, :VH], ALU.add)
+        nc.vector.tensor_tensor(num[:, VH:], energy2[:], power[:, VH:], ALU.add)
+        nc.scalar.activation(ln_den[:, :VH], sums1[:, 1, :], ACT.Ln, bias=0.1 * LN_SHIFT, scale=20.0 * LN_SHIFT)
         ln_num = sb.tile([P, V], F32, name="ln_num")
         nc.scalar.activation(ln_num[:], num[:], ACT.Ln, bias=0.005 * LN_SHIFT, scale=LN_SHIFT)
         result = sb.tile([P, V], F32, name="result")

@@ -47,25 +47,31 @@ def tile_picked_ydas_log_p_kernel(tc, x_words, x_scales, w1, apo, offs, out):
         x_planes = sb.tile([P, PASSES * S], U8, name="x_planes", align_bytes=64)
         nc.vector.memset(x_planes[:].bitcast(I32), 0)
 
-        w_raw = sb.tile([P, PASSES, 4, M], F32, name="w_raw", tag="w_then_table")
-        nc.sync.dma_start(
-            w_raw[:].rearrange("p o t m -> p o (t m)"),
-            w1.rearrange("(o p t) m -> p o (t m)", o=PASSES, t=4),
-        )
+        w_rows = w1.rearrange("(o p t) m -> o p (t m)", o=PASSES, t=4)
+        w_codes = sb.tile([P, PASSES * M], U32, name="w_codes", align_bytes=64)
+        w_plane = sb.tile([P, PASSES * M], U8, name="w_plane", align_bytes=64)
+
+        def quantise(o, grouped):
+            nc.vector.quantize_mx(
+                out=w_codes[:, o * M : (o + 1) * M].bitcast(FP8X4),
+                scales=w_plane[:, o * M : (o + 1) * M],
+                in_=grouped[:].rearrange("p m t -> p (m t)"),
+            )
+
+        w_raw0 = sb.tile([P, 4, M], F32, name="w_raw0", tag="w_then_table")
+        nc.sync.dma_start(w_raw0[:].rearrange("p t m -> p (t m)"), w_rows[0])
         nc.sync.dma_start(offsets[:], offs)
         word_table0 = sb.tile([P, T], I32, name="word_table0")
         nc.sync.dma_start(word_table0[:], x_words[0].rearrange("p c r -> p (c r)").bitcast(I32))
 
-        w_grouped = sb.tile([P, PASSES, M, 4], BF16, name="w_grouped", align_bytes=64)
-        nc.vector.tensor_copy(w_grouped[:], w_raw[:].rearrange("p o t m -> p o m t"))
-        w_codes = sb.tile([P, PASSES * M], U32, name="w_codes", align_bytes=64)
-        w_plane = sb.tile([P, PASSES * M], U8, name="w_plane", align_bytes=64)
-        nc.vector.quantize_mx(
-            out=w_codes[:].bitcast(FP8X4), scales=w_plane[:], in_=w_grouped[:].rearrange("p o m t -> p (o m t)")
-        )
+        w_grouped0 = sb.tile([P, M, 4], BF16, name="w_grouped0", tag="late_weights", align_bytes=64)
+        nc.vector.tensor_copy(w_grouped0[:], w_raw0[:].rearrange("p t m -> p m t"))
+        quantise(0, w_grouped0)
         word_table1 = sb.tile([P, T], I32, name="word_table1", tag="w_then_table")
         nc.sync.dma_start(word_table1[:], x_words[1].rearrange("p c r -> p (c r)").bitcast(I32))
         word_tables = [word_table0, word_table1]
+        w_raw1 = sb.tile([P, 4, M], F32, name="w_raw1", tag="late_weights", align_bytes=64)
+        nc.sync.dma_start(w_raw1[:].rearrange("p t m -> p (t m)"), w_rows[1])
 
         ln_warm = sb.tile([P, 1], F32, name="ln_warm")
         nc.scalar.activation(ln_warm[:], apo_vd[:, 0:1], ACT.Ln, bias=1.0, scale=0.0)
@@ -104,11 +110,18 @@ def tile_picked_ydas_log_p_kernel(tc, x_words, x_scales, w1, apo, offs, out):
                 stop=(o == PASSES - 1),
             )
 
+        w_grouped1 = sb.tile([P, M, 4], BF16, name="w_grouped1", align_bytes=64)
+        nc.scalar.copy(
+            w_grouped1[:].rearrange("p (c i) t -> p c t i", i=4), w_raw1[:].rearrange("p t (c i) -> p c t i", i=4)
+        )
+
         y = [ps.tile([P, QUARTER], F32, name=f"y{c}") for c in range(4)]
         for h in range(2):
-            picked1 = sb.tile([P, HALF], U32, name=f"picked1_{h}", align_bytes=64)
+            picked1 = sb.tile([P, HALF], U32, name=f"picked1_{h}", tag=("first_half", "late_weights")[h], align_bytes=64)
             cols = slice(h * HALF // 16, (h + 1) * HALF // 16)
             nc.vector.tensor_copy(picked1[:], word_tables[1][:].bitcast(U32).indirect(offsets[:, cols]))
+            if h == 0:
+                quantise(1, w_grouped1)
             for c in (2 * h, 2 * h + 1):
                 product(y[c], 0, c, picked0[:, c * QUARTER : (c + 1) * QUARTER])
             for i in range(2):

@@ -129,7 +129,7 @@ def tile_picked_ydas_log_p_kernel(tc, x_words, x_scales, w1, apo, offs, out):
 
         y_dv = [y[c][:].rearrange("p (v d) -> p d v", d=D) for c in range(4)]
         y_vd = [y[c][:].rearrange("p (v d) -> p v d", d=D) for c in range(4)]
-        stacked = sb.tile([P, D, 2, VH], F32, name="stacked")
+        stacked = sb.tile([P, D, 2, VH], F32, name="stacked", tag="stacked_then_late")
         y_sum = sb.tile([P, V], F32, name="y_sum")
         for c in range(2):
             nc.scalar.activation(stacked[:, :, 1, c * VQ : (c + 1) * VQ], y_dv[c], ACT.Square, scale=SQ_SCALE)
@@ -149,10 +149,15 @@ def tile_picked_ydas_log_p_kernel(tc, x_words, x_scales, w1, apo, offs, out):
         for c in range(2):
             nc.vector.tensor_reduce(y_sum[:, c * VQ : (c + 1) * VQ], y_vd[c], AX.X, ALU.add)
 
-        sq = sb.tile([P, VH, D], F32, name="sq")
+        sq = sb.tile([P, 2, VH, D // 2], F32, name="sq")
         ys = sb.tile([P, VH, D], F32, name="ys")
         for c in range(2):
-            nc.scalar.activation(sq[:, c * VQ : (c + 1) * VQ, :], y_vd[2 + c], ACT.Square, scale=SQ_SCALE)
+            nc.scalar.activation(
+                sq[:, :, c * VQ : (c + 1) * VQ, :],
+                y[2 + c][:].rearrange("p (v u e) -> p u v e", u=2, e=D // 2),
+                ACT.Square,
+                scale=SQ_SCALE,
+            )
         for c in range(2):
             vs = slice(c * VQ, (c + 1) * VQ)
             nc.vector.tensor_tensor(ys[:, vs, :], y_vd[2 + c], apo_vd2[:, vs, :], ALU.mult)
@@ -162,29 +167,30 @@ def tile_picked_ydas_log_p_kernel(tc, x_words, x_scales, w1, apo, offs, out):
         nc.vector.tensor_reduce(beam2[:], ys[:], AX.X, ALU.add)
 
         energy2 = sb.tile([P, VH], F32, name="energy2")
-        nc.vector.tensor_reduce(energy2[:], sq[:], AX.X, ALU.add)
+        sq_pairs = sb.tile([P, VH, D // 2], F32, name="sq_pairs")
+        nc.gpsimd.tensor_tensor(sq_pairs[:], sq[:, 0], sq[:, 1], ALU.add)
+        nc.vector.tensor_reduce(energy2[:], sq_pairs[:], AX.X, ALU.add)
 
         abs_t = sb.tile([P, M], F32, name="abs_t")
         nc.scalar.activation(abs_t[:], sums_t[:], ACT.Abs)
         sums1 = ps.tile([P, 2, VH], F32, name="sums1")
         nc.tensor.transpose(sums1[:].rearrange("p s v -> p (s v)"), abs_t[:], ident[:])
 
-        sum_sq = sb.tile([P, V], F32, name="sum_sq")
-        nc.scalar.activation(sum_sq[:], y_sum[:], ACT.Square)
-        beam2_abs = sb.tile([P, VH], F32, name="beam2_abs")
-        nc.scalar.activation(beam2_abs[:], beam2[:], ACT.Abs)
-        ln_den = sb.tile([P, V], F32, name="ln_den")
+        late = sb.tile([P, 2 * V + VH], F32, name="late", tag="stacked_then_late")
+        sum_sq, ln_den, beam2_abs = late[:, :V], late[:, V : 2 * V], late[:, 2 * V :]
+        nc.scalar.activation(sum_sq, y_sum[:], ACT.Square)
+        nc.scalar.activation(beam2_abs, beam2[:], ACT.Abs)
         nc.scalar.activation(ln_den[:, VH:], energy2[:], ACT.Ln, bias=0.1 * LN_SHIFT, scale=20.0 * LN_SHIFT)
 
         power = sb.tile([P, V], F32, name="power")
         num = sb.tile([P, V], F32, name="num")
         nc.vector.tensor_tensor(power[:, :VH], sums1[:, 0, :], sum_sq[:, :VH], ALU.mult)
-        nc.vector.tensor_tensor(power[:, VH:], beam2_abs[:], sum_sq[:, VH:], ALU.mult)
+        nc.vector.tensor_tensor(power[:, VH:], beam2_abs, sum_sq[:, VH:], ALU.mult)
         nc.vector.tensor_tensor(num[:, :VH], sums1[:, 1, :], power[:, :VH], ALU.add)
         nc.vector.tensor_tensor(num[:, VH:], energy2[:], power[:, VH:], ALU.add)
         nc.scalar.activation(ln_den[:, :VH], sums1[:, 1, :], ACT.Ln, bias=0.1 * LN_SHIFT, scale=20.0 * LN_SHIFT)
         ln_num = sb.tile([P, V], F32, name="ln_num")
         nc.scalar.activation(ln_num[:], num[:], ACT.Ln, bias=0.005 * LN_SHIFT, scale=LN_SHIFT)
         result = sb.tile([P, V], F32, name="result")
-        nc.vector.tensor_tensor(result[:], ln_num[:], ln_den[:], ALU.subtract)
+        nc.vector.tensor_tensor(result[:], ln_num[:], ln_den, ALU.subtract)
         nc.sync.dma_start(out, result[:])

@@ -78,14 +78,14 @@ def tile_picked_ydas_log_p_kernel(tc, x_words, x_scales, w1, apo, offs, out):
 
         ident = sb.tile([P, P], F32, name="ident")
         make_identity(nc, ident[:])
-        apo_dv = sb.tile([P, D, VH], F32, name="apo_dv")
+        apo_dv = sb.tile([P, 2, D, VQ], F32, name="apo_dv", tag="apo_then_ys")
         apo_vd2 = sb.tile([P, VH, D], F32, name="apo_vd2")
         for g in range(2):
-            apo_ps = ps.tile([P, 4, V], F32, name=f"apo_ps{g}")
+            apo_ps = ps.tile([P, 4, V], F32, name=f"apo_ps{g}", tag=f"spread{g}")
             for i in range(4):
                 d = 4 * g + i
                 nc.tensor.transpose(apo_ps[:, i, :], apo_vd[:, d : d + 1].to_broadcast([P, P]), ident[:])
-            nc.scalar.copy(apo_dv[:, 4 * g : 4 * g + 4, :], apo_ps[:, :, :VH])
+            nc.scalar.copy(apo_dv[:, :, 4 * g : 4 * g + 4, :], apo_ps[:, :, :VH].rearrange("p d (c v) -> p c d v", c=2))
             nc.scalar.copy(apo_vd2[:, :, 4 * g : 4 * g + 4], apo_ps[:, :, VH:].rearrange("p d v -> p v d"))
 
         picked_scales = sb.tile([P, S], U8, name="picked_scales")
@@ -131,11 +131,13 @@ def tile_picked_ydas_log_p_kernel(tc, x_words, x_scales, w1, apo, offs, out):
         y_vd = [y[c][:].rearrange("p (v d) -> p v d", d=D) for c in range(4)]
         stacked = sb.tile([P, D, 2, VH], F32, name="stacked", tag="stacked_then_late")
         y_sum = sb.tile([P, V], F32, name="y_sum")
+        y_first = sb.tile([P, D, VQ], F32, name="y_first")
+        nc.scalar.copy(y_first[:], y_dv[0])
+        nc.gpsimd.tensor_tensor(stacked[:, :, 0, :VQ], y_first[:], apo_dv[:, 0], ALU.mult)
         for c in range(2):
             nc.scalar.activation(stacked[:, :, 1, c * VQ : (c + 1) * VQ], y_dv[c], ACT.Square, scale=SQ_SCALE)
-        for c in range(2):
-            vs = slice(c * VQ, (c + 1) * VQ)
-            nc.vector.tensor_tensor(stacked[:, :, 0, vs], y_dv[c], apo_dv[:, :, vs], ALU.mult)
+        nc.vector.tensor_reduce(y_sum[:, :VQ], y_vd[0], AX.X, ALU.add)
+        nc.vector.tensor_tensor(stacked[:, :, 0, VQ:], y_dv[1], apo_dv[:, 1], ALU.mult)
         sums_t = ps.tile([P, M], F32, name="sums_t")
         for d in range(D):
             nc.tensor.matmul(
@@ -146,49 +148,60 @@ def tile_picked_ydas_log_p_kernel(tc, x_words, x_scales, w1, apo, offs, out):
                 stop=(d == D - 1),
                 is_transpose=True,
             )
-        for c in range(2):
-            nc.vector.tensor_reduce(y_sum[:, c * VQ : (c + 1) * VQ], y_vd[c], AX.X, ALU.add)
+        nc.vector.tensor_reduce(y_sum[:, VQ:VH], y_vd[1], AX.X, ALU.add)
 
-        sq = sb.tile([P, 2, VH, D // 2], F32, name="sq")
-        ys = sb.tile([P, VH, D], F32, name="ys")
-        for c in range(2):
+        sq = sb.tile([P, 2, 2, VQ, D // 2], F32, name="sq", tag="sq_then_power")
+        sq_pairs = sb.tile([P, 2, VQ, D // 2], F32, name="sq_pairs")
+        ys = sb.tile([P, VH, D], F32, name="ys", tag="apo_then_ys")
+
+        def square(c):
             nc.scalar.activation(
-                sq[:, :, c * VQ : (c + 1) * VQ, :],
+                sq[:, c],
                 y[2 + c][:].rearrange("p (v u e) -> p u v e", u=2, e=D // 2),
                 ACT.Square,
                 scale=SQ_SCALE,
             )
-        for c in range(2):
+            nc.gpsimd.tensor_tensor(sq_pairs[:, c], sq[:, c, 0], sq[:, c, 1], ALU.add)
+
+        def weigh(c):
             vs = slice(c * VQ, (c + 1) * VQ)
             nc.vector.tensor_tensor(ys[:, vs, :], y_vd[2 + c], apo_vd2[:, vs, :], ALU.mult)
-        for c in range(2):
-            nc.vector.tensor_reduce(y_sum[:, VH + c * VQ : VH + (c + 1) * VQ], y_vd[2 + c], AX.X, ALU.add)
+
+        square(0)
+        weigh(1)
+        weigh(0)
+        square(1)
+        sum_sq1 = sb.tile([P, VH], F32, name="sum_sq1")
+        nc.scalar.activation(sum_sq1[:], y_sum[:, :VH], ACT.Square)
+        nc.vector.tensor_reduce(y_sum[:, VH : VH + VQ], y_vd[2], AX.X, ALU.add)
         beam2 = sb.tile([P, VH], F32, name="beam2")
         nc.vector.tensor_reduce(beam2[:], ys[:], AX.X, ALU.add)
+        nc.vector.tensor_reduce(y_sum[:, VH + VQ :], y_vd[3], AX.X, ALU.add)
 
         energy2 = sb.tile([P, VH], F32, name="energy2")
-        sq_pairs = sb.tile([P, VH, D // 2], F32, name="sq_pairs")
-        nc.gpsimd.tensor_tensor(sq_pairs[:], sq[:, 0], sq[:, 1], ALU.add)
-        nc.vector.tensor_reduce(energy2[:], sq_pairs[:], AX.X, ALU.add)
+        nc.vector.tensor_reduce(energy2[:], sq_pairs[:].rearrange("p c v e -> p (c v) e"), AX.X, ALU.add)
 
         abs_t = sb.tile([P, M], F32, name="abs_t")
         nc.scalar.activation(abs_t[:], sums_t[:], ACT.Abs)
         sums1 = ps.tile([P, 2, VH], F32, name="sums1")
         nc.tensor.transpose(sums1[:].rearrange("p s v -> p (s v)"), abs_t[:], ident[:])
+        sums1_again = ps.tile([P, 2, VH], F32, name="sums1_again", tag="spread0")
+        nc.tensor.transpose(sums1_again[:].rearrange("p s v -> p (s v)"), abs_t[:], ident[:])
 
-        late = sb.tile([P, 2 * V + VH], F32, name="late", tag="stacked_then_late")
-        sum_sq, ln_den, beam2_abs = late[:, :V], late[:, V : 2 * V], late[:, 2 * V :]
-        nc.scalar.activation(sum_sq, y_sum[:], ACT.Square)
+        late = sb.tile([P, V + VH], F32, name="late", tag="stacked_then_late")
+        ln_den, beam2_abs = late[:, :V], late[:, V:]
         nc.scalar.activation(beam2_abs, beam2[:], ACT.Abs)
         nc.scalar.activation(ln_den[:, VH:], energy2[:], ACT.Ln, bias=0.1 * LN_SHIFT, scale=20.0 * LN_SHIFT)
+        nc.scalar.activation(ln_den[:, :VH], sums1_again[:, 1, :], ACT.Ln, bias=0.1 * LN_SHIFT, scale=20.0 * LN_SHIFT)
 
-        power = sb.tile([P, V], F32, name="power")
+        power = sb.tile([P, V], F32, name="power", tag="sq_then_power")
         num = sb.tile([P, V], F32, name="num")
-        nc.vector.tensor_tensor(power[:, :VH], sums1[:, 0, :], sum_sq[:, :VH], ALU.mult)
-        nc.vector.tensor_tensor(power[:, VH:], beam2_abs, sum_sq[:, VH:], ALU.mult)
+        half_power = sb.tile([P, VH], F32, name="half_power")
+        nc.vector.tensor_tensor(half_power[:], beam2_abs, y_sum[:, VH:], ALU.mult)
+        nc.vector.tensor_tensor(power[:, :VH], sums1[:, 0, :], sum_sq1[:], ALU.mult)
+        nc.vector.tensor_tensor(power[:, VH:], half_power[:], y_sum[:, VH:], ALU.mult)
         nc.vector.tensor_tensor(num[:, :VH], sums1[:, 1, :], power[:, :VH], ALU.add)
         nc.vector.tensor_tensor(num[:, VH:], energy2[:], power[:, VH:], ALU.add)
-        nc.scalar.activation(ln_den[:, :VH], sums1[:, 1, :], ACT.Ln, bias=0.1 * LN_SHIFT, scale=20.0 * LN_SHIFT)
         ln_num = sb.tile([P, V], F32, name="ln_num")
         nc.scalar.activation(ln_num[:], num[:], ACT.Ln, bias=0.005 * LN_SHIFT, scale=LN_SHIFT)
         result = sb.tile([P, V], F32, name="result")

@@ -130,14 +130,16 @@ def tile_picked_ydas_log_p_kernel(tc, x_words, x_scales, w1, apo, offs, out):
         y_dv = [y[c][:].rearrange("p (v d) -> p d v", d=D) for c in range(4)]
         y_vd = [y[c][:].rearrange("p (v d) -> p v d", d=D) for c in range(4)]
         stacked = sb.tile([P, D, 2, VH], F32, name="stacked", tag="stacked_then_late")
-        y_sum = sb.tile([P, V], F32, name="y_sum")
-        y_first = sb.tile([P, D, VQ], F32, name="y_first")
-        nc.scalar.copy(y_first[:], y_dv[0])
-        nc.gpsimd.tensor_tensor(stacked[:, :, 0, :VQ], y_first[:], apo_dv[:, 0], ALU.mult)
-        for c in range(2):
+        y_sum1 = sb.tile([P, VH], F32, name="y_sum1")
+        y_first = sb.tile([P, D * VQ], F32, name="y_first")
+        nc.scalar.copy(y_first[:].rearrange("p (d v) -> p d v", d=D), y_dv[0])
+        nc.gpsimd.tensor_tensor(
+            stacked[:, :, 0, :VQ], y_first[:].rearrange("p (d v) -> p d v", d=D), apo_dv[:, 0], ALU.mult
+        )
+        for c in (1, 0):
             nc.scalar.activation(stacked[:, :, 1, c * VQ : (c + 1) * VQ], y_dv[c], ACT.Square, scale=SQ_SCALE)
-        nc.vector.tensor_reduce(y_sum[:, :VQ], y_vd[0], AX.X, ALU.add)
         nc.vector.tensor_tensor(stacked[:, :, 0, VQ:], y_dv[1], apo_dv[:, 1], ALU.mult)
+        nc.vector.tensor_reduce(y_sum1[:, VQ:], y_vd[1], AX.X, ALU.add)
         sums_t = ps.tile([P, M], F32, name="sums_t")
         for d in range(D):
             nc.tensor.matmul(
@@ -148,38 +150,36 @@ def tile_picked_ydas_log_p_kernel(tc, x_words, x_scales, w1, apo, offs, out):
                 stop=(d == D - 1),
                 is_transpose=True,
             )
-        nc.vector.tensor_reduce(y_sum[:, VQ:VH], y_vd[1], AX.X, ALU.add)
+        four = sb.tile([P, 4 * VQ], F32, name="four")
+        two = sb.tile([P, 2 * VQ], F32, name="two")
+        nc.gpsimd.tensor_tensor(four[:], y_first[:, : 4 * VQ], y_first[:, 4 * VQ :], ALU.add)
+        nc.gpsimd.tensor_tensor(two[:], four[:, : 2 * VQ], four[:, 2 * VQ :], ALU.add)
+        nc.gpsimd.tensor_tensor(y_sum1[:, :VQ], two[:, :VQ], two[:, VQ:], ALU.add)
 
-        sq = sb.tile([P, 2, 2, VQ, D // 2], F32, name="sq", tag="sq_then_power")
-        sq_pairs = sb.tile([P, 2, VQ, D // 2], F32, name="sq_pairs")
-        ys = sb.tile([P, VH, D], F32, name="ys", tag="apo_then_ys")
+        sq_third = sb.tile([P, VQ, D], F32, name="sq_third")
+        sq_last = sb.tile([P, 2, VQ, D // 2], F32, name="sq_last", tag="sq_then_power")
+        sq_pairs = sb.tile([P, VQ, D // 2], F32, name="sq_pairs")
+        second = sb.tile([P, HALF + VH], F32, name="second", tag="apo_then_ys")
+        ys = second[:, :HALF].rearrange("p (v d) -> p v d", d=D)
+        y_sum2 = second[:, HALF:]
 
-        def square(c):
-            nc.scalar.activation(
-                sq[:, c],
-                y[2 + c][:].rearrange("p (v u e) -> p u v e", u=2, e=D // 2),
-                ACT.Square,
-                scale=SQ_SCALE,
-            )
-            nc.gpsimd.tensor_tensor(sq_pairs[:, c], sq[:, c, 0], sq[:, c, 1], ALU.add)
-
-        def weigh(c):
+        def weigh_and_sum(c):
             vs = slice(c * VQ, (c + 1) * VQ)
             nc.vector.tensor_tensor(ys[:, vs, :], y_vd[2 + c], apo_vd2[:, vs, :], ALU.mult)
+            nc.vector.tensor_reduce(y_sum2[:, vs], y_vd[2 + c], AX.X, ALU.add)
 
-        square(0)
-        weigh(1)
-        weigh(0)
-        square(1)
-        sum_sq1 = sb.tile([P, VH], F32, name="sum_sq1")
-        nc.scalar.activation(sum_sq1[:], y_sum[:, :VH], ACT.Square)
-        nc.vector.tensor_reduce(y_sum[:, VH : VH + VQ], y_vd[2], AX.X, ALU.add)
+        nc.scalar.activation(
+            sq_last[:], y[3][:].rearrange("p (v u e) -> p u v e", u=2, e=D // 2), ACT.Square, scale=SQ_SCALE
+        )
+        nc.gpsimd.tensor_tensor(sq_pairs[:], sq_last[:, 0], sq_last[:, 1], ALU.add)
+        weigh_and_sum(0)
+        nc.scalar.activation(sq_third[:], y_vd[2], ACT.Square, scale=SQ_SCALE)
+        weigh_and_sum(1)
         beam2 = sb.tile([P, VH], F32, name="beam2")
-        nc.vector.tensor_reduce(beam2[:], ys[:], AX.X, ALU.add)
-        nc.vector.tensor_reduce(y_sum[:, VH + VQ :], y_vd[3], AX.X, ALU.add)
-
+        nc.vector.tensor_reduce(beam2[:], ys, AX.X, ALU.add)
         energy2 = sb.tile([P, VH], F32, name="energy2")
-        nc.vector.tensor_reduce(energy2[:], sq_pairs[:].rearrange("p c v e -> p (c v) e"), AX.X, ALU.add)
+        nc.vector.tensor_reduce(energy2[:, :VQ], sq_third[:], AX.X, ALU.add)
+        nc.vector.tensor_reduce(energy2[:, VQ:], sq_pairs[:], AX.X, ALU.add)
 
         abs_t = sb.tile([P, M], F32, name="abs_t")
         nc.scalar.activation(abs_t[:], sums_t[:], ACT.Abs)
@@ -188,20 +188,20 @@ def tile_picked_ydas_log_p_kernel(tc, x_words, x_scales, w1, apo, offs, out):
         sums1_again = ps.tile([P, 2, VH], F32, name="sums1_again", tag="spread0")
         nc.tensor.transpose(sums1_again[:].rearrange("p s v -> p (s v)"), abs_t[:], ident[:])
 
-        late = sb.tile([P, V + VH], F32, name="late", tag="stacked_then_late")
-        ln_den, beam2_abs = late[:, :V], late[:, V:]
+        late = sb.tile([P, 2 * V + VH], F32, name="late", tag="stacked_then_late")
+        sum_sq, ln_den, beam2_abs = late[:, :V], late[:, V : 2 * V], late[:, 2 * V :]
+        nc.scalar.activation(sum_sq[:, VH:], y_sum2, ACT.Square)
         nc.scalar.activation(beam2_abs, beam2[:], ACT.Abs)
+        nc.scalar.activation(sum_sq[:, :VH], y_sum1[:], ACT.Square)
         nc.scalar.activation(ln_den[:, VH:], energy2[:], ACT.Ln, bias=0.1 * LN_SHIFT, scale=20.0 * LN_SHIFT)
         nc.scalar.activation(ln_den[:, :VH], sums1_again[:, 1, :], ACT.Ln, bias=0.1 * LN_SHIFT, scale=20.0 * LN_SHIFT)
 
         power = sb.tile([P, V], F32, name="power", tag="sq_then_power")
         num = sb.tile([P, V], F32, name="num")
-        half_power = sb.tile([P, VH], F32, name="half_power")
-        nc.vector.tensor_tensor(half_power[:], beam2_abs, y_sum[:, VH:], ALU.mult)
-        nc.vector.tensor_tensor(power[:, :VH], sums1[:, 0, :], sum_sq1[:], ALU.mult)
-        nc.vector.tensor_tensor(power[:, VH:], half_power[:], y_sum[:, VH:], ALU.mult)
-        nc.vector.tensor_tensor(num[:, :VH], sums1[:, 1, :], power[:, :VH], ALU.add)
+        nc.vector.tensor_tensor(power[:, VH:], beam2_abs, sum_sq[:, VH:], ALU.mult)
+        nc.vector.tensor_tensor(power[:, :VH], sums1[:, 0, :], sum_sq[:, :VH], ALU.mult)
         nc.vector.tensor_tensor(num[:, VH:], energy2[:], power[:, VH:], ALU.add)
+        nc.vector.tensor_tensor(num[:, :VH], sums1[:, 1, :], power[:, :VH], ALU.add)
         ln_num = sb.tile([P, V], F32, name="ln_num")
         nc.scalar.activation(ln_num[:], num[:], ACT.Ln, bias=0.005 * LN_SHIFT, scale=LN_SHIFT)
         result = sb.tile([P, V], F32, name="result")

@@ -203,7 +203,8 @@ def tile_picked_ydas_log_p_kernel(tc, x_words, x_scales, w1, apo, offs, out):
         nc.vector.tensor_tensor(num[:, VH:], energy2[:], power[:, VH:], ALU.add)
         nc.vector.tensor_tensor(num[:, :VH], sums1[:, 1, :], power[:, :VH], ALU.add)
         ln_num = sb.tile([P, V], F32, name="ln_num")
-        nc.scalar.activation(ln_num[:], num[:], ACT.Ln, bias=0.005 * LN_SHIFT, scale=LN_SHIFT)
         result = sb.tile([P, V], F32, name="result")
-        nc.vector.tensor_tensor(result[:], ln_num[:], ln_den, ALU.subtract)
+        for vs in (slice(VH, V), slice(0, VH)):
+            nc.scalar.activation(ln_num[:, vs], num[:, vs], ACT.Ln, bias=0.005 * LN_SHIFT, scale=LN_SHIFT)
+            nc.vector.tensor_tensor(result[:, vs], ln_num[:, vs], ln_den[:, vs], ALU.subtract)
         nc.sync.dma_start(out, result[:])

@@ -36,14 +36,10 @@ def tile_picked_ydas_log_p_kernel(tc, x_words, x_scales, w1, apo, offs, out):
 
         offsets = sb.tile([P, S // 16], U16, name="offsets")
         apo_vd = sb.tile([P, D], F32, name="apo_vd")
-        nc.scalar.dma_start(apo_vd[:], apo[0:1, :].rearrange("o (v d) -> (o v) d", d=D))
 
         scale_table = sb.tile([P, T], U8, name="scale_table", tag="scales_then_words", align_bytes=64)
-        nc.vector.memset(scale_table[:].bitcast(I32), 0)
-        nc.scalar.dma_start(
-            scale_table[:].bitcast(I32)[0:P:4, :],
-            x_scales.bitcast(I32).rearrange("o q c -> q o c"),
-        )
+        nc.gpsimd.memset(scale_table[:].bitcast(I32)[:, : T // 8], 0)
+        nc.vector.memset(scale_table[:].bitcast(I32)[:, T // 8 :], 0)
         x_planes = sb.tile([P, PASSES * S], U8, name="x_planes", align_bytes=64)
         nc.vector.memset(x_planes[:].bitcast(I32), 0)
 
@@ -58,19 +54,25 @@ def tile_picked_ydas_log_p_kernel(tc, x_words, x_scales, w1, apo, offs, out):
                 in_=grouped[:].rearrange("p m t -> p (m t)"),
             )
 
-        w_raw0 = sb.tile([P, 4, M], F32, name="w_raw0", tag="w_then_table")
+        placed = ctx.enter_context(tc.tile_pool(name="placed", bufs=1))
+        w_raw0 = placed.tile([P, 4, M], F32, name="w_raw0", offset=4 * T - 1024)
         nc.sync.dma_start(w_raw0[:].rearrange("p t m -> p (t m)"), w_rows[0])
         nc.sync.dma_start(offsets[:], offs)
+        nc.sync.dma_start(apo_vd[:], apo[0:1, :].rearrange("o (v d) -> (o v) d", d=D))
+        nc.sync.dma_start(
+            scale_table[:].bitcast(I32)[0:P:4, :],
+            x_scales.bitcast(I32).rearrange("o q c -> q o c"),
+        )
         word_table0 = sb.tile([P, T], I32, name="word_table0")
         nc.sync.dma_start(word_table0[:], x_words[0].rearrange("p c r -> p (c r)").bitcast(I32))
 
-        w_grouped0 = sb.tile([P, M, 4], BF16, name="w_grouped0", tag="late_weights", align_bytes=64)
+        w_grouped0 = sb.tile([P, M, 4], BF16, name="w_grouped0", align_bytes=64)
         nc.vector.tensor_copy(w_grouped0[:], w_raw0[:].rearrange("p t m -> p m t"))
         quantise(0, w_grouped0)
-        word_table1 = sb.tile([P, T], I32, name="word_table1", tag="w_then_table")
+        word_table1 = placed.tile([P, T], I32, name="word_table1", offset=0)
         nc.sync.dma_start(word_table1[:], x_words[1].rearrange("p c r -> p (c r)").bitcast(I32))
         word_tables = [word_table0, word_table1]
-        w_raw1 = sb.tile([P, 4, M], F32, name="w_raw1", tag="late_weights", align_bytes=64)
+        w_raw1 = placed.tile([P, 4, M], F32, name="w_raw1", offset=4 * T)
         nc.sync.dma_start(w_raw1[:].rearrange("p t m -> p (t m)"), w_rows[1])
 
         ln_warm = sb.tile([P, 1], F32, name="ln_warm")
@@ -117,7 +119,10 @@ def tile_picked_ydas_log_p_kernel(tc, x_words, x_scales, w1, apo, offs, out):
 
         y = [ps.tile([P, QUARTER], F32, name=f"y{c}") for c in range(4)]
         for h in range(2):
-            picked1 = sb.tile([P, HALF], U32, name=f"picked1_{h}", tag=("first_half", "late_weights")[h], align_bytes=64)
+            if h == 0:
+                picked1 = sb.tile([P, HALF], U32, name="picked1_0", align_bytes=64)
+            else:
+                picked1 = placed.tile([P, HALF], U32, name="picked1_1", offset=4 * T + 1024)
             cols = slice(h * HALF // 16, (h + 1) * HALF // 16)
             nc.vector.tensor_copy(picked1[:], word_tables[1][:].bitcast(U32).indirect(offsets[:, cols]))
             if h == 0:

@@ -57,14 +57,16 @@ def tile_picked_ydas_log_p_kernel(tc, x_words, x_scales, w1, apo, offs, out):
         placed = ctx.enter_context(tc.tile_pool(name="placed", bufs=1))
         w_raw0 = placed.tile([P, 4, M], F32, name="w_raw0", offset=4 * T - 1024)
         nc.sync.dma_start(w_raw0[:].rearrange("p t m -> p (t m)"), w_rows[0])
+        word_table0 = sb.tile([P, T], I32, name="word_table0")
+        words0 = x_words[0].rearrange("p c r -> p (c r)").bitcast(I32)
+        nc.sync.dma_start(word_table0[:, : T // 4], words0[:, : T // 4])
         nc.sync.dma_start(offsets[:], offs)
         nc.sync.dma_start(apo_vd[:], apo[0:1, :].rearrange("o (v d) -> (o v) d", d=D))
         nc.sync.dma_start(
             scale_table[:].bitcast(I32)[0:P:4, :],
             x_scales.bitcast(I32).rearrange("o q c -> q o c"),
         )
-        word_table0 = sb.tile([P, T], I32, name="word_table0")
-        nc.sync.dma_start(word_table0[:], x_words[0].rearrange("p c r -> p (c r)").bitcast(I32))
+        nc.sync.dma_start(word_table0[:, T // 4 :], words0[:, T // 4 :])
 
         w_grouped0 = sb.tile([P, M, 4], BF16, name="w_grouped0", align_bytes=64)
         nc.vector.tensor_copy(w_grouped0[:], w_raw0[:].rearrange("p t m -> p m t"))

@@ -82,14 +82,17 @@ def tile_picked_ydas_log_p_kernel(tc, x_words, x_scales, w1, apo, offs, out):
 
         ident = sb.tile([P, P], F32, name="ident")
         make_identity(nc, ident[:])
-        apo_dv = sb.tile([P, 2, D, VQ], F32, name="apo_dv", tag="apo_then_ys")
+        apo_dv0 = sb.tile([P, D, VQ], F32, name="apo_dv0", tag="apo_then_ys")
+        apo_dv1 = sb.tile([P, D, VQ], F32, name="apo_dv1")
+        apo_dv = [apo_dv0, apo_dv1]
         apo_vd2 = sb.tile([P, VH, D], F32, name="apo_vd2")
         for g in range(2):
             apo_ps = ps.tile([P, 4, V], F32, name=f"apo_ps{g}", tag=f"spread{g}")
             for i in range(4):
                 d = 4 * g + i
                 nc.tensor.transpose(apo_ps[:, i, :], apo_vd[:, d : d + 1].to_broadcast([P, P]), ident[:])
-            nc.scalar.copy(apo_dv[:, :, 4 * g : 4 * g + 4, :], apo_ps[:, :, :VH].rearrange("p d (c v) -> p c d v", c=2))
+            for c in range(2):
+                nc.scalar.copy(apo_dv[c][:, 4 * g : 4 * g + 4, :], apo_ps[:, :, c * VQ : (c + 1) * VQ])
             nc.scalar.copy(apo_vd2[:, :, 4 * g : 4 * g + 4], apo_ps[:, :, VH:].rearrange("p d v -> p v d"))
 
         picked_scales = sb.tile([P, S], U8, name="picked_scales")
@@ -129,24 +132,23 @@ def tile_picked_ydas_log_p_kernel(tc, x_words, x_scales, w1, apo, offs, out):
             nc.vector.tensor_copy(picked1[:], word_tables[1][:].bitcast(U32).indirect(offsets[:, cols]))
             if h == 0:
                 quantise(1, w_grouped1)
-            for c in (2 * h, 2 * h + 1):
-                product(y[c], 0, c, picked0[:, c * QUARTER : (c + 1) * QUARTER])
-            for i in range(2):
-                product(y[2 * h + i], 1, 2 * h + i, picked1[:, i * QUARTER : (i + 1) * QUARTER])
+            steps = [(0, 0), (0, 1), (1, 0), (1, 1)] if h == 0 else [(0, 0), (1, 0), (0, 1), (1, 1)]
+            for o, i in steps:
+                c = 2 * h + i
+                source = picked1[:, i * QUARTER : (i + 1) * QUARTER] if o else picked0[:, c * QUARTER : (c + 1) * QUARTER]
+                product(y[c], o, c, source)
 
         y_dv = [y[c][:].rearrange("p (v d) -> p d v", d=D) for c in range(4)]
         y_vd = [y[c][:].rearrange("p (v d) -> p v d", d=D) for c in range(4)]
         stacked = sb.tile([P, D, 2, VH], F32, name="stacked", tag="stacked_then_late")
         y_sum1 = sb.tile([P, VH], F32, name="y_sum1")
-        y_first = sb.tile([P, D * VQ], F32, name="y_first")
-        nc.scalar.copy(y_first[:].rearrange("p (d v) -> p d v", d=D), y_dv[0])
-        nc.gpsimd.tensor_tensor(
-            stacked[:, :, 0, :VQ], y_first[:].rearrange("p (d v) -> p d v", d=D), apo_dv[:, 0], ALU.mult
-        )
-        for c in (1, 0):
-            nc.scalar.activation(stacked[:, :, 1, c * VQ : (c + 1) * VQ], y_dv[c], ACT.Square, scale=SQ_SCALE)
-        nc.vector.tensor_tensor(stacked[:, :, 0, VQ:], y_dv[1], apo_dv[:, 1], ALU.mult)
-        nc.vector.tensor_reduce(y_sum1[:, VQ:], y_vd[1], AX.X, ALU.add)
+        y_first = sb.tile([P, D, VH], F32, name="y_first")
+        for c in range(2):
+            nc.scalar.copy(y_first[:, :, c * VQ : (c + 1) * VQ], y_dv[c])
+            nc.vector.tensor_tensor(stacked[:, :, 0, c * VQ : (c + 1) * VQ], y_dv[c], apo_dv[c][:], ALU.mult)
+        for c in range(2):
+            vs = slice(c * VQ, (c + 1) * VQ)
+            nc.scalar.activation(stacked[:, :, 1, vs], y_first[:, :, vs], ACT.Square, scale=SQ_SCALE)
         sums_t = ps.tile([P, M], F32, name="sums_t")
         for d in range(D):
             nc.tensor.matmul(
@@ -157,11 +159,11 @@ def tile_picked_ydas_log_p_kernel(tc, x_words, x_scales, w1, apo, offs, out):
                 stop=(d == D - 1),
                 is_transpose=True,
             )
-        four = sb.tile([P, 4 * VQ], F32, name="four")
-        two = sb.tile([P, 2 * VQ], F32, name="two")
-        nc.gpsimd.tensor_tensor(four[:], y_first[:, : 4 * VQ], y_first[:, 4 * VQ :], ALU.add)
-        nc.gpsimd.tensor_tensor(two[:], four[:, : 2 * VQ], four[:, 2 * VQ :], ALU.add)
-        nc.gpsimd.tensor_tensor(y_sum1[:, :VQ], two[:, :VQ], two[:, VQ:], ALU.add)
+        four = sb.tile([P, 4, VH], F32, name="four")
+        two = sb.tile([P, 2, VH], F32, name="two")
+        nc.gpsimd.tensor_tensor(four[:], y_first[:, :4], y_first[:, 4:], ALU.add)
+        nc.gpsimd.tensor_tensor(two[:], four[:, :2], four[:, 2:], ALU.add)
+        nc.gpsimd.tensor_tensor(y_sum1[:], two[:, 0], two[:, 1], ALU.add)
 
         sq_third = sb.tile([P, VQ, D], F32, name="sq_third")
         sq_last = sb.tile([P, 2, VQ, D // 2], F32, name="sq_last", tag="sq_then_power")
@@ -169,11 +171,13 @@ def tile_picked_ydas_log_p_kernel(tc, x_words, x_scales, w1, apo, offs, out):
         second = sb.tile([P, HALF + VH], F32, name="second", tag="apo_then_ys")
         ys = second[:, :HALF].rearrange("p (v d) -> p v d", d=D)
         y_sum2 = second[:, HALF:]
+        beam2 = sb.tile([P, VH], F32, name="beam2")
 
         def weigh_and_sum(c):
             vs = slice(c * VQ, (c + 1) * VQ)
             nc.vector.tensor_tensor(ys[:, vs, :], y_vd[2 + c], apo_vd2[:, vs, :], ALU.mult)
             nc.vector.tensor_reduce(y_sum2[:, vs], y_vd[2 + c], AX.X, ALU.add)
+            nc.vector.tensor_reduce(beam2[:, vs], ys[:, vs, :], AX.X, ALU.add)
 
         nc.scalar.activation(
             sq_last[:], y[3][:].rearrange("p (v u e) -> p u v e", u=2, e=D // 2), ACT.Square, scale=SQ_SCALE
@@ -182,8 +186,6 @@ def tile_picked_ydas_log_p_kernel(tc, x_words, x_scales, w1, apo, offs, out):
         weigh_and_sum(0)
         nc.scalar.activation(sq_third[:], y_vd[2], ACT.Square, scale=SQ_SCALE)
         weigh_and_sum(1)
-        beam2 = sb.tile([P, VH], F32, name="beam2")
-        nc.vector.tensor_reduce(beam2[:], ys, AX.X, ALU.add)
         energy2 = sb.tile([P, VH], F32, name="energy2")
         nc.vector.tensor_reduce(energy2[:, :VQ], sq_third[:], AX.X, ALU.add)
         nc.vector.tensor_reduce(energy2[:, VQ:], sq_pairs[:], AX.X, ALU.add)

@@ -26,6 +26,7 @@ ACT = mybir.ActivationFunctionType
 AX = mybir.AxisListType
 LN_SHIFT = 2.0 ** -32
 SQ_SCALE = 0.4 ** 0.5
+EARLY_WORDS = 7 * T // 16
 
 
 def tile_picked_ydas_log_p_kernel(tc, x_words, x_scales, w1, apo, offs, out):
@@ -55,26 +56,26 @@ def tile_picked_ydas_log_p_kernel(tc, x_words, x_scales, w1, apo, offs, out):
             )
 
         placed = ctx.enter_context(tc.tile_pool(name="placed", bufs=1))
-        w_raw0 = placed.tile([P, 4, M], F32, name="w_raw0", offset=4 * T - 1024)
+        w_raw0 = placed.tile([P, 4, M], F32, name="w_raw0", offset=0)
         nc.sync.dma_start(w_raw0[:].rearrange("p t m -> p (t m)"), w_rows[0])
         word_table0 = sb.tile([P, T], I32, name="word_table0")
-        words0 = x_words[0].rearrange("p c r -> p (c r)").bitcast(I32)
-        nc.sync.dma_start(word_table0[:, : T // 4], words0[:, : T // 4])
+        word_table1 = sb.tile([P, T], I32, name="word_table1")
+        words1 = x_words[1].rearrange("p c r -> p (c r)").bitcast(I32)
+        nc.sync.dma_start(word_table1[:, :EARLY_WORDS], words1[:, :EARLY_WORDS])
         nc.sync.dma_start(offsets[:], offs)
         nc.sync.dma_start(apo_vd[:], apo[0:1, :].rearrange("o (v d) -> (o v) d", d=D))
         nc.sync.dma_start(
             scale_table[:].bitcast(I32)[0:P:4, :],
             x_scales.bitcast(I32).rearrange("o q c -> q o c"),
         )
-        nc.sync.dma_start(word_table0[:, T // 4 :], words0[:, T // 4 :])
+        nc.sync.dma_start(word_table0[:], x_words[0].rearrange("p c r -> p (c r)").bitcast(I32))
+        nc.sync.dma_start(word_table1[:, EARLY_WORDS:], words1[:, EARLY_WORDS:])
 
         w_grouped0 = sb.tile([P, M, 4], BF16, name="w_grouped0", align_bytes=64)
         nc.vector.tensor_copy(w_grouped0[:], w_raw0[:].rearrange("p t m -> p m t"))
         quantise(0, w_grouped0)
-        word_table1 = placed.tile([P, T], I32, name="word_table1", offset=0)
-        nc.sync.dma_start(word_table1[:], x_words[1].rearrange("p c r -> p (c r)").bitcast(I32))
         word_tables = [word_table0, word_table1]
-        w_raw1 = placed.tile([P, 4, M], F32, name="w_raw1", offset=4 * T)
+        w_raw1 = placed.tile([P, 4, M], F32, name="w_raw1", offset=1024)
         nc.sync.dma_start(w_raw1[:].rearrange("p t m -> p (t m)"), w_rows[1])
 
         ln_warm = sb.tile([P, 1], F32, name="ln_warm")
@@ -127,7 +128,7 @@ def tile_picked_ydas_log_p_kernel(tc, x_words, x_scales, w1, apo, offs, out):
             if h == 0:
                 picked1 = sb.tile([P, HALF], U32, name="picked1_0", align_bytes=64)
             else:
-                picked1 = placed.tile([P, HALF], U32, name="picked1_1", offset=4 * T + 1024)
+                picked1 = placed.tile([P, HALF], U32, name="picked1_1", offset=2048)
             cols = slice(h * HALF // 16, (h + 1) * HALF // 16)
             nc.vector.tensor_copy(picked1[:], word_tables[1][:].bitcast(U32).indirect(offsets[:, cols]))
             if h == 0:
@@ -145,10 +146,13 @@ def tile_picked_ydas_log_p_kernel(tc, x_words, x_scales, w1, apo, offs, out):
         y_first = sb.tile([P, D, VH], F32, name="y_first")
         for c in range(2):
             nc.scalar.copy(y_first[:, :, c * VQ : (c + 1) * VQ], y_dv[c])
-            nc.vector.tensor_tensor(stacked[:, :, 0, c * VQ : (c + 1) * VQ], y_dv[c], apo_dv[c][:], ALU.mult)
-        for c in range(2):
-            vs = slice(c * VQ, (c + 1) * VQ)
-            nc.scalar.activation(stacked[:, :, 1, vs], y_first[:, :, vs], ACT.Square, scale=SQ_SCALE)
+            for ds in (slice(0, D),) if c == 0 else (slice(0, D // 2), slice(D // 2, D)):
+                nc.vector.tensor_tensor(
+                    stacked[:, ds, 0, c * VQ : (c + 1) * VQ], y_dv[c][:, ds], apo_dv[c][:, ds], ALU.mult
+                )
+        nc.scalar.activation(stacked[:, :, 1, :VQ], y_first[:, :, :VQ], ACT.Square, scale=SQ_SCALE)
+        for ds in (slice(0, D // 2), slice(D // 2, D)):
+            nc.scalar.activation(stacked[:, ds, 1, VQ:], y_first[:, ds, VQ:], ACT.Square, scale=SQ_SCALE)
         sums_t = ps.tile([P, M], F32, name="sums_t")
         for d in range(D):
             nc.tensor.matmul(

@@ -96,7 +96,7 @@ def tile_picked_ydas_log_p_kernel(tc, x_words, x_scales, w1, apo, offs, out):
                 nc.scalar.copy(apo_dv[c][:, 4 * g : 4 * g + 4, :], apo_ps[:, :, c * VQ : (c + 1) * VQ])
             nc.scalar.copy(apo_vd2[:, :, 4 * g : 4 * g + 4], apo_ps[:, :, VH:].rearrange("p d v -> p v d"))
 
-        picked_scales = sb.tile([P, S], U8, name="picked_scales")
+        picked_scales = sb.tile([P, S], U8, name="picked_scales", align_bytes=64)
         nc.vector.tensor_copy(picked_scales[:], scale_table[:].indirect(offsets[:]))
         for q in range(4):
             nc.sync.dma_start(
@@ -117,6 +117,17 @@ def tile_picked_ydas_log_p_kernel(tc, x_words, x_scales, w1, apo, offs, out):
                 start=(o == 0),
                 stop=(o == PASSES - 1),
             )
+
+        warm = ps.tile([P, HALF], F32, name="warm", tag="spread1")
+        nc.tensor.matmul_mx(
+            out=warm[:],
+            lhsT=w_codes[:, :M].bitcast(FP8X4),
+            lhsT_scale=w_plane[:, :M],
+            rhs=picked0[:, :HALF].bitcast(FP8X4),
+            rhs_scale=picked_scales[:, :HALF],
+            start=True,
+            stop=True,
+        )
 
         w_grouped1 = sb.tile([P, M, 4], BF16, name="w_grouped1", align_bytes=64)
         nc.scalar.copy(

@@ -27,6 +27,7 @@ AX = mybir.AxisListType
 LN_SHIFT = 2.0 ** -32
 SQ_SCALE = 0.4 ** 0.5
 EARLY_WORDS = 7 * T // 16
+AHEAD = 640
 
 
 def tile_picked_ydas_log_p_kernel(tc, x_words, x_scales, w1, apo, offs, out):
@@ -107,27 +108,17 @@ def tile_picked_ydas_log_p_kernel(tc, x_words, x_scales, w1, apo, offs, out):
         picked0 = sb.tile([P, S], U32, name="picked0", tag="scales_then_words", align_bytes=64)
         nc.vector.tensor_copy(picked0[:], word_tables[0][:].bitcast(U32).indirect(offsets[:]))
 
-        def product(bank, o, c, picked):
+        def product(first, n, o, picked, stop):
+            c = first // QUARTER
             nc.tensor.matmul_mx(
-                out=bank[:],
+                out=y[c][:, first - c * QUARTER : first - c * QUARTER + n],
                 lhsT=w_codes[:, o * M : (o + 1) * M].bitcast(FP8X4),
                 lhsT_scale=w_plane[:, o * M : (o + 1) * M],
                 rhs=picked.bitcast(FP8X4),
-                rhs_scale=x_planes[:, o * S + c * QUARTER : o * S + (c + 1) * QUARTER],
+                rhs_scale=x_planes[:, o * S + first : o * S + first + n],
                 start=(o == 0),
-                stop=(o == PASSES - 1),
+                stop=stop,
             )
-
-        warm = ps.tile([P, HALF], F32, name="warm", tag="spread1")
-        nc.tensor.matmul_mx(
-            out=warm[:],
-            lhsT=w_codes[:, :M].bitcast(FP8X4),
-            lhsT_scale=w_plane[:, :M],
-            rhs=picked0[:, :HALF].bitcast(FP8X4),
-            rhs_scale=picked_scales[:, :HALF],
-            start=True,
-            stop=True,
-        )
 
         w_grouped1 = sb.tile([P, M, 4], BF16, name="w_grouped1", align_bytes=64)
         nc.scalar.copy(
@@ -135,20 +126,24 @@ def tile_picked_ydas_log_p_kernel(tc, x_words, x_scales, w1, apo, offs, out):
         )
 
         y = [ps.tile([P, QUARTER], F32, name=f"y{c}") for c in range(4)]
-        for h in range(2):
-            if h == 0:
-                picked1 = sb.tile([P, HALF], U32, name="picked1_0", align_bytes=64)
-            else:
-                picked1 = placed.tile([P, HALF], U32, name="picked1_1", offset=2048)
-            cols = slice(h * HALF // 16, (h + 1) * HALF // 16)
-            nc.vector.tensor_copy(picked1[:], word_tables[1][:].bitcast(U32).indirect(offsets[:, cols]))
-            if h == 0:
-                quantise(1, w_grouped1)
-            steps = [(0, 0), (0, 1), (1, 0), (1, 1)] if h == 0 else [(0, 0), (1, 0), (0, 1), (1, 1)]
-            for o, i in steps:
-                c = 2 * h + i
-                source = picked1[:, i * QUARTER : (i + 1) * QUARTER] if o else picked0[:, c * QUARTER : (c + 1) * QUARTER]
-                product(y[c], o, c, source)
+
+        def pass0(c):
+            product(c * QUARTER, QUARTER, 0, picked0[:, c * QUARTER : (c + 1) * QUARTER], False)
+
+        picked1a = sb.tile([P, AHEAD], U32, name="picked1a", align_bytes=64)
+        nc.vector.tensor_copy(picked1a[:], word_tables[1][:].bitcast(U32).indirect(offsets[:, : AHEAD // 16]))
+        quantise(1, w_grouped1)
+        pass0(0)
+        pass0(1)
+        for c in range(2):
+            product(c * QUARTER, QUARTER, 1, picked1a[:, c * QUARTER : (c + 1) * QUARTER], True)
+        pass0(2)
+        product(HALF, AHEAD - HALF, 1, picked1a[:, HALF:], False)
+        picked1b = placed.tile([P, S - AHEAD], U32, name="picked1b", offset=2048)
+        nc.vector.tensor_copy(picked1b[:], word_tables[1][:].bitcast(U32).indirect(offsets[:, AHEAD // 16 :]))
+        product(AHEAD, 3 * QUARTER - AHEAD, 1, picked1b[:, : 3 * QUARTER - AHEAD], True)
+        pass0(3)
+        product(3 * QUARTER, QUARTER, 1, picked1b[:, 3 * QUARTER - AHEAD :], True)
 
         y_dv = [y[c][:].rearrange("p (v d) -> p d v", d=D) for c in range(4)]
         y_vd = [y[c][:].rearrange("p (v d) -> p v d", d=D) for c in range(4)]

@@ -26,8 +26,6 @@ ACT = mybir.ActivationFunctionType
 AX = mybir.AxisListType
 LN_SHIFT = 2.0 ** -32
 SQ_SCALE = 0.4 ** 0.5
-EARLY_WORDS = 7 * T // 16
-AHEAD = 640
 
 
 def tile_picked_ydas_log_p_kernel(tc, x_words, x_scales, w1, apo, offs, out):
@@ -45,39 +43,27 @@ def tile_picked_ydas_log_p_kernel(tc, x_words, x_scales, w1, apo, offs, out):
         x_planes = sb.tile([P, PASSES * S], U8, name="x_planes", align_bytes=64)
         nc.vector.memset(x_planes[:].bitcast(I32), 0)
 
-        w_rows = w1.rearrange("(o p t) m -> o p (t m)", o=PASSES, t=4)
-        w_codes = sb.tile([P, PASSES * M], U32, name="w_codes", align_bytes=64)
-        w_plane = sb.tile([P, PASSES * M], U8, name="w_plane", align_bytes=64)
-
-        def quantise(o, grouped):
-            nc.vector.quantize_mx(
-                out=w_codes[:, o * M : (o + 1) * M].bitcast(FP8X4),
-                scales=w_plane[:, o * M : (o + 1) * M],
-                in_=grouped[:].rearrange("p m t -> p (m t)"),
-            )
-
-        placed = ctx.enter_context(tc.tile_pool(name="placed", bufs=1))
-        w_raw0 = placed.tile([P, 4, M], F32, name="w_raw0", offset=0)
-        nc.sync.dma_start(w_raw0[:].rearrange("p t m -> p (t m)"), w_rows[0])
-        word_table0 = sb.tile([P, T], I32, name="word_table0")
-        word_table1 = sb.tile([P, T], I32, name="word_table1")
-        words1 = x_words[1].rearrange("p c r -> p (c r)").bitcast(I32)
-        nc.sync.dma_start(word_table1[:, :EARLY_WORDS], words1[:, :EARLY_WORDS])
+        w_raw = sb.tile([P, PASSES, 4, M], F32, name="w_raw")
+        nc.sync.dma_start(
+            w_raw[:].rearrange("p o t m -> p o (t m)"), w1.rearrange("(o p t) m -> p o (t m)", o=PASSES, t=4)
+        )
         nc.sync.dma_start(offsets[:], offs)
         nc.sync.dma_start(apo_vd[:], apo[0:1, :].rearrange("o (v d) -> (o v) d", d=D))
         nc.sync.dma_start(
             scale_table[:].bitcast(I32)[0:P:4, :],
             x_scales.bitcast(I32).rearrange("o q c -> q o c"),
         )
-        nc.sync.dma_start(word_table0[:], x_words[0].rearrange("p c r -> p (c r)").bitcast(I32))
-        nc.sync.dma_start(word_table1[:, EARLY_WORDS:], words1[:, EARLY_WORDS:])
+        word_tables = [sb.tile([P, T], I32, name=f"word_table{o}") for o in range(PASSES)]
+        for o in range(PASSES):
+            nc.sync.dma_start(word_tables[o][:], x_words[o].rearrange("p c r -> p (c r)").bitcast(I32))
 
-        w_grouped0 = sb.tile([P, M, 4], BF16, name="w_grouped0", align_bytes=64)
-        nc.vector.tensor_copy(w_grouped0[:], w_raw0[:].rearrange("p t m -> p m t"))
-        quantise(0, w_grouped0)
-        word_tables = [word_table0, word_table1]
-        w_raw1 = placed.tile([P, 4, M], F32, name="w_raw1", offset=1024)
-        nc.sync.dma_start(w_raw1[:].rearrange("p t m -> p (t m)"), w_rows[1])
+        w_grouped = sb.tile([P, PASSES, M, 4], BF16, name="w_grouped", align_bytes=64)
+        nc.vector.tensor_copy(w_grouped[:], w_raw[:].rearrange("p o t m -> p o m t"))
+        w_codes = sb.tile([P, PASSES * M], U32, name="w_codes", align_bytes=64)
+        w_plane = sb.tile([P, PASSES * M], U8, name="w_plane", align_bytes=64)
+        nc.vector.quantize_mx(
+            out=w_codes[:].bitcast(FP8X4), scales=w_plane[:], in_=w_grouped[:].rearrange("p o m t -> p (o m t)")
+        )
 
         ln_warm = sb.tile([P, 1], F32, name="ln_warm")
         nc.scalar.activation(ln_warm[:], apo_vd[:, 0:1], ACT.Ln, bias=1.0, scale=0.0)
@@ -99,7 +85,7 @@ def tile_picked_ydas_log_p_kernel(tc, x_words, x_scales, w1, apo, offs, out):
 
         picked_scales = sb.tile([P, S], U8, name="picked_scales", align_bytes=64)
         nc.vector.tensor_copy(picked_scales[:], scale_table[:].indirect(offsets[:]))
-        for q in range(4):
+        for q in (0, 2, 1, 3):
             nc.sync.dma_start(
                 x_planes[:].bitcast(I32)[32 * q : 32 * q + 4, :],
                 picked_scales[:].bitcast(I32)[32 * q : 32 * q + 32 : 4, :],
@@ -108,42 +94,24 @@ def tile_picked_ydas_log_p_kernel(tc, x_words, x_scales, w1, apo, offs, out):
         picked0 = sb.tile([P, S], U32, name="picked0", tag="scales_then_words", align_bytes=64)
         nc.vector.tensor_copy(picked0[:], word_tables[0][:].bitcast(U32).indirect(offsets[:]))
 
-        def product(first, n, o, picked, stop):
-            c = first // QUARTER
-            nc.tensor.matmul_mx(
-                out=y[c][:, first - c * QUARTER : first - c * QUARTER + n],
-                lhsT=w_codes[:, o * M : (o + 1) * M].bitcast(FP8X4),
-                lhsT_scale=w_plane[:, o * M : (o + 1) * M],
-                rhs=picked.bitcast(FP8X4),
-                rhs_scale=x_planes[:, o * S + first : o * S + first + n],
-                start=(o == 0),
-                stop=stop,
-            )
-
-        w_grouped1 = sb.tile([P, M, 4], BF16, name="w_grouped1", align_bytes=64)
-        nc.scalar.copy(
-            w_grouped1[:].rearrange("p (c i) t -> p c t i", i=4), w_raw1[:].rearrange("p t (c i) -> p c t i", i=4)
-        )
-
         y = [ps.tile([P, QUARTER], F32, name=f"y{c}") for c in range(4)]
-
-        def pass0(c):
-            product(c * QUARTER, QUARTER, 0, picked0[:, c * QUARTER : (c + 1) * QUARTER], False)
-
-        picked1a = sb.tile([P, AHEAD], U32, name="picked1a", align_bytes=64)
-        nc.vector.tensor_copy(picked1a[:], word_tables[1][:].bitcast(U32).indirect(offsets[:, : AHEAD // 16]))
-        quantise(1, w_grouped1)
-        pass0(0)
-        pass0(1)
-        for c in range(2):
-            product(c * QUARTER, QUARTER, 1, picked1a[:, c * QUARTER : (c + 1) * QUARTER], True)
-        pass0(2)
-        product(HALF, AHEAD - HALF, 1, picked1a[:, HALF:], False)
-        picked1b = placed.tile([P, S - AHEAD], U32, name="picked1b", offset=2048)
-        nc.vector.tensor_copy(picked1b[:], word_tables[1][:].bitcast(U32).indirect(offsets[:, AHEAD // 16 :]))
-        product(AHEAD, 3 * QUARTER - AHEAD, 1, picked1b[:, : 3 * QUARTER - AHEAD], True)
-        pass0(3)
-        product(3 * QUARTER, QUARTER, 1, picked1b[:, 3 * QUARTER - AHEAD :], True)
+        picked1 = sb.tile([P, S], U32, name="picked1", align_bytes=64)
+        for c in range(4):
+            cols = slice(c * QUARTER, (c + 1) * QUARTER)
+            nc.vector.tensor_copy(
+                picked1[:, cols],
+                word_tables[1][:].bitcast(U32).indirect(offsets[:, c * QUARTER // 16 : (c + 1) * QUARTER // 16]),
+            )
+            for o, picked in enumerate((picked0, picked1)):
+                nc.tensor.matmul_mx(
+                    out=y[c][:],
+                    lhsT=w_codes[:, o * M : (o + 1) * M].bitcast(FP8X4),
+                    lhsT_scale=w_plane[:, o * M : (o + 1) * M],
+                    rhs=picked[:, cols].bitcast(FP8X4),
+                    rhs_scale=x_planes[:, o * S + c * QUARTER : o * S + (c + 1) * QUARTER],
+                    start=(o == 0),
+                    stop=(o == PASSES - 1),
+                )
 
         y_dv = [y[c][:].rearrange("p (v d) -> p d v", d=D) for c in range(4)]
         y_vd = [y[c][:].rearrange("p (v d) -> p v d", d=D) for c in range(4)]

@@ -70,9 +70,9 @@ def tile_picked_ydas_log_p_kernel(tc, x_words, x_scales, w1, apo, offs, out):
 
         ident = sb.tile([P, P], F32, name="ident")
         make_identity(nc, ident[:])
-        apo_dv0 = sb.tile([P, D, VQ], F32, name="apo_dv0", tag="apo_then_ys")
-        apo_dv1 = sb.tile([P, D, VQ], F32, name="apo_dv1")
-        apo_dv = [apo_dv0, apo_dv1]
+        apo_dv = [
+            [sb.tile([P, 4, VQ], F32, name=f"apo_dv{c}{g}", tag=f"apo_dv{c}{g}") for g in range(2)] for c in range(2)
+        ]
         apo_vd2 = sb.tile([P, VH, D], F32, name="apo_vd2")
         for g in range(2):
             apo_ps = ps.tile([P, 4, V], F32, name=f"apo_ps{g}", tag=f"spread{g}")
@@ -80,7 +80,7 @@ def tile_picked_ydas_log_p_kernel(tc, x_words, x_scales, w1, apo, offs, out):
                 d = 4 * g + i
                 nc.tensor.transpose(apo_ps[:, i, :], apo_vd[:, d : d + 1].to_broadcast([P, P]), ident[:])
             for c in range(2):
-                nc.scalar.copy(apo_dv[c][:, 4 * g : 4 * g + 4, :], apo_ps[:, :, c * VQ : (c + 1) * VQ])
+                nc.scalar.copy(apo_dv[c][g][:], apo_ps[:, :, c * VQ : (c + 1) * VQ])
             nc.scalar.copy(apo_vd2[:, :, 4 * g : 4 * g + 4], apo_ps[:, :, VH:].rearrange("p d v -> p v d"))
 
         picked_scales = sb.tile([P, S], U8, name="picked_scales", align_bytes=64)
@@ -117,16 +117,21 @@ def tile_picked_ydas_log_p_kernel(tc, x_words, x_scales, w1, apo, offs, out):
         y_vd = [y[c][:].rearrange("p (v d) -> p v d", d=D) for c in range(4)]
         stacked = sb.tile([P, D, 2, VH], F32, name="stacked", tag="stacked_then_late")
         y_sum1 = sb.tile([P, VH], F32, name="y_sum1")
-        y_first = sb.tile([P, D, VH], F32, name="y_first")
-        for c in range(2):
-            nc.scalar.copy(y_first[:, :, c * VQ : (c + 1) * VQ], y_dv[c])
-            for ds in (slice(0, D),) if c == 0 else (slice(0, D // 2), slice(D // 2, D)):
-                nc.vector.tensor_tensor(
-                    stacked[:, ds, 0, c * VQ : (c + 1) * VQ], y_dv[c][:, ds], apo_dv[c][:, ds], ALU.mult
-                )
-        nc.scalar.activation(stacked[:, :, 1, :VQ], y_first[:, :, :VQ], ACT.Square, scale=SQ_SCALE)
-        for ds in (slice(0, D // 2), slice(D // 2, D)):
-            nc.scalar.activation(stacked[:, ds, 1, VQ:], y_first[:, ds, VQ:], ACT.Square, scale=SQ_SCALE)
+        y_first = [sb.tile([P, D, VQ], F32, name=f"y_first{c}", tag=("copy_sq_power", "copy1")[c]) for c in range(2)]
+        four = sb.tile([P, 4, VH], F32, name="four")
+        two = sb.tile([P, 2, VH], F32, name="two")
+        low, high = slice(0, D // 2), slice(D // 2, D)
+        nc.scalar.copy(y_first[0][:], y_dv[0])
+        nc.scalar.activation(stacked[:, low, 1, :VQ], y_dv[0][:, low], ACT.Square, scale=SQ_SCALE)
+        for g, ds in enumerate((low, high)):
+            nc.vector.tensor_tensor(stacked[:, ds, 0, :VQ], y_dv[0][:, ds], apo_dv[0][g][:], ALU.mult)
+        nc.gpsimd.tensor_tensor(four[:, :, :VQ], y_first[0][:, low], y_first[0][:, high], ALU.add)
+        nc.scalar.copy(y_first[1][:], y_dv[1])
+        nc.scalar.activation(stacked[:, high, 1, :VQ], y_first[0][:, high], ACT.Square, scale=SQ_SCALE)
+        for g, ds in enumerate((low, high)):
+            nc.vector.tensor_tensor(stacked[:, ds, 0, VQ:], y_dv[1][:, ds], apo_dv[1][g][:], ALU.mult)
+            nc.scalar.activation(stacked[:, ds, 1, VQ:], y_first[1][:, ds], ACT.Square, scale=SQ_SCALE)
+        nc.gpsimd.tensor_tensor(four[:, :, VQ:], y_first[1][:, low], y_first[1][:, high], ALU.add)
         sums_t = ps.tile([P, M], F32, name="sums_t")
         for d in range(D):
             nc.tensor.matmul(
@@ -137,16 +142,13 @@ def tile_picked_ydas_log_p_kernel(tc, x_words, x_scales, w1, apo, offs, out):
                 stop=(d == D - 1),
                 is_transpose=True,
             )
-        four = sb.tile([P, 4, VH], F32, name="four")
-        two = sb.tile([P, 2, VH], F32, name="two")
-        nc.gpsimd.tensor_tensor(four[:], y_first[:, :4], y_first[:, 4:], ALU.add)
         nc.gpsimd.tensor_tensor(two[:], four[:, :2], four[:, 2:], ALU.add)
         nc.gpsimd.tensor_tensor(y_sum1[:], two[:, 0], two[:, 1], ALU.add)
 
         sq_third = sb.tile([P, VQ, D], F32, name="sq_third")
-        sq_last = sb.tile([P, 2, VQ, D // 2], F32, name="sq_last", tag="sq_then_power")
+        sq_last = sb.tile([P, 2, VQ, D // 2], F32, name="sq_last", tag="copy_sq_power")
         sq_pairs = sb.tile([P, VQ, D // 2], F32, name="sq_pairs")
-        second = sb.tile([P, HALF + VH], F32, name="second", tag="apo_then_ys")
+        second = sb.tile([P, HALF + VH], F32, name="second", tag="apo_dv00")
         ys = second[:, :HALF].rearrange("p (v d) -> p v d", d=D)
         y_sum2 = second[:, HALF:]
         beam2 = sb.tile([P, VH], F32, name="beam2")
@@ -178,20 +180,20 @@ def tile_picked_ydas_log_p_kernel(tc, x_words, x_scales, w1, apo, offs, out):
         late = sb.tile([P, 2 * V + VH], F32, name="late", tag="stacked_then_late")
         sum_sq, ln_den, beam2_abs = late[:, :V], late[:, V : 2 * V], late[:, 2 * V :]
         nc.scalar.activation(sum_sq[:, VH:], y_sum2, ACT.Square)
-        nc.scalar.activation(beam2_abs, beam2[:], ACT.Abs)
         nc.scalar.activation(sum_sq[:, :VH], y_sum1[:], ACT.Square)
+        nc.scalar.activation(beam2_abs, beam2[:], ACT.Abs)
         nc.scalar.activation(ln_den[:, VH:], energy2[:], ACT.Ln, bias=0.1 * LN_SHIFT, scale=20.0 * LN_SHIFT)
         nc.scalar.activation(ln_den[:, :VH], sums1_again[:, 1, :], ACT.Ln, bias=0.1 * LN_SHIFT, scale=20.0 * LN_SHIFT)
 
-        power = sb.tile([P, V], F32, name="power", tag="sq_then_power")
+        power = sb.tile([P, V], F32, name="power", tag="copy_sq_power")
         num = sb.tile([P, V], F32, name="num")
-        nc.vector.tensor_tensor(power[:, VH:], beam2_abs, sum_sq[:, VH:], ALU.mult)
         nc.vector.tensor_tensor(power[:, :VH], sums1[:, 0, :], sum_sq[:, :VH], ALU.mult)
-        nc.vector.tensor_tensor(num[:, VH:], energy2[:], power[:, VH:], ALU.add)
+        nc.vector.tensor_tensor(power[:, VH:], beam2_abs, sum_sq[:, VH:], ALU.mult)
         nc.vector.tensor_tensor(num[:, :VH], sums1[:, 1, :], power[:, :VH], ALU.add)
+        nc.vector.tensor_tensor(num[:, VH:], energy2[:], power[:, VH:], ALU.add)
         ln_num = sb.tile([P, V], F32, name="ln_num")
         result = sb.tile([P, V], F32, name="result")
-        for vs in (slice(VH, V), slice(0, VH)):
+        for vs in (slice(0, VH), slice(VH, V)):
             nc.scalar.activation(ln_num[:, vs], num[:, vs], ACT.Ln, bias=0.005 * LN_SHIFT, scale=LN_SHIFT)
             nc.vector.tensor_tensor(result[:, vs], ln_num[:, vs], ln_den[:, vs], ALU.subtract)
         nc.sync.dma_start(out, result[:])

@@ -11,6 +11,8 @@ HALF = S // 2
 VH = V // 2
 QUARTER = S // 4
 VQ = V // 4
+EIGHTH = S // 8
+VE = V // 8
 FLOPS = 2 * K * M * S
 BYTES = K * T + K // 32 * T + K * M * 4 + S * 4 + P * S // 16 * 2 + M * V * 4
 
@@ -73,7 +75,7 @@ def tile_picked_ydas_log_p_kernel(tc, x_words, x_scales, w1, apo, offs, out):
         apo_dv = [
             [sb.tile([P, 4, VQ], F32, name=f"apo_dv{c}{g}", tag=f"apo_dv{c}{g}") for g in range(2)] for c in range(2)
         ]
-        apo_vd2 = sb.tile([P, VH, D], F32, name="apo_vd2")
+        apo_vd2 = sb.tile([P, VH, D], F32, name="apo_vd2", tag="apo_then_energy")
         for g in range(2):
             apo_ps = ps.tile([P, 4, V], F32, name=f"apo_ps{g}", tag=f"spread{g}")
             for i in range(4):
@@ -94,27 +96,33 @@ def tile_picked_ydas_log_p_kernel(tc, x_words, x_scales, w1, apo, offs, out):
         picked0 = sb.tile([P, S], U32, name="picked0", tag="scales_then_words", align_bytes=64)
         nc.vector.tensor_copy(picked0[:], word_tables[0][:].bitcast(U32).indirect(offsets[:]))
 
-        y = [ps.tile([P, QUARTER], F32, name=f"y{c}") for c in range(4)]
+        widths = {0: QUARTER, QUARTER: QUARTER, HALF: QUARTER, 6 * EIGHTH: EIGHTH, 7 * EIGHTH: EIGHTH}
+        y = {first: ps.tile([P, n], F32, name=f"y{first}", tag=f"y{first}") for first, n in widths.items()}
         picked1 = sb.tile([P, S], U32, name="picked1", align_bytes=64)
+
+        def product(first, o, picked):
+            cols = slice(first, first + widths[first])
+            nc.tensor.matmul_mx(
+                out=y[first][:],
+                lhsT=w_codes[:, o * M : (o + 1) * M].bitcast(FP8X4),
+                lhsT_scale=w_plane[:, o * M : (o + 1) * M],
+                rhs=picked[:, cols].bitcast(FP8X4),
+                rhs_scale=x_planes[:, o * S + first : o * S + first + widths[first]],
+                start=(o == 0),
+                stop=(o == PASSES - 1),
+            )
+
         for c in range(4):
-            cols = slice(c * QUARTER, (c + 1) * QUARTER)
             nc.vector.tensor_copy(
-                picked1[:, cols],
+                picked1[:, c * QUARTER : (c + 1) * QUARTER],
                 word_tables[1][:].bitcast(U32).indirect(offsets[:, c * QUARTER // 16 : (c + 1) * QUARTER // 16]),
             )
             for o, picked in enumerate((picked0, picked1)):
-                nc.tensor.matmul_mx(
-                    out=y[c][:],
-                    lhsT=w_codes[:, o * M : (o + 1) * M].bitcast(FP8X4),
-                    lhsT_scale=w_plane[:, o * M : (o + 1) * M],
-                    rhs=picked[:, cols].bitcast(FP8X4),
-                    rhs_scale=x_planes[:, o * S + c * QUARTER : o * S + (c + 1) * QUARTER],
-                    start=(o == 0),
-                    stop=(o == PASSES - 1),
-                )
+                for first in widths:
+                    if first // QUARTER == c:
+                        product(first, o, picked)
 
-        y_dv = [y[c][:].rearrange("p (v d) -> p d v", d=D) for c in range(4)]
-        y_vd = [y[c][:].rearrange("p (v d) -> p v d", d=D) for c in range(4)]
+        y_dv = [y[c * QUARTER][:].rearrange("p (v d) -> p d v", d=D) for c in range(2)]
         stacked = sb.tile([P, D, 2, VH], F32, name="stacked", tag="stacked_then_late")
         y_sum1 = sb.tile([P, VH], F32, name="y_sum1")
         y_first = [sb.tile([P, D, VQ], F32, name=f"y_first{c}", tag=("copy_sq_power", "copy1")[c]) for c in range(2)]
@@ -153,26 +161,34 @@ def tile_picked_ydas_log_p_kernel(tc, x_words, x_scales, w1, apo, offs, out):
         y_sum2 = second[:, HALF:]
         beam2 = sb.tile([P, VH], F32, name="beam2")
 
-        def weigh_and_sum(c):
-            vs = slice(c * VQ, (c + 1) * VQ)
-            nc.vector.tensor_tensor(ys[:, vs, :], y_vd[2 + c], apo_vd2[:, vs, :], ALU.mult)
-            nc.vector.tensor_reduce(y_sum2[:, vs], y_vd[2 + c], AX.X, ALU.add)
-            nc.vector.tensor_reduce(beam2[:, vs], ys[:, vs, :], AX.X, ALU.add)
+        def weigh_and_sum(first):
+            vs = slice((first - HALF) // D, (first - HALF + widths[first]) // D)
+            y_vd = y[first][:].rearrange("p (v d) -> p v d", d=D)
+            nc.vector.tensor_tensor(ys[:, vs, :], y_vd, apo_vd2[:, vs, :], ALU.mult)
+            nc.vector.tensor_reduce(y_sum2[:, vs], y_vd, AX.X, ALU.add)
 
-        nc.scalar.activation(
-            sq_last[:], y[3][:].rearrange("p (v u e) -> p u v e", u=2, e=D // 2), ACT.Square, scale=SQ_SCALE
-        )
+        for i in range(2):
+            nc.scalar.activation(
+                sq_last[:, :, i * VE : (i + 1) * VE],
+                y[(6 + i) * EIGHTH][:].rearrange("p (v u e) -> p u v e", u=2, e=D // 2),
+                ACT.Square,
+                scale=SQ_SCALE,
+            )
         nc.gpsimd.tensor_tensor(sq_pairs[:], sq_last[:, 0], sq_last[:, 1], ALU.add)
-        weigh_and_sum(0)
-        nc.scalar.activation(sq_third[:], y_vd[2], ACT.Square, scale=SQ_SCALE)
-        weigh_and_sum(1)
-        energy2 = sb.tile([P, VH], F32, name="energy2")
+        weigh_and_sum(HALF)
+        nc.vector.tensor_reduce(beam2[:, :VQ], ys[:, :VQ, :], AX.X, ALU.add)
+        nc.scalar.activation(sq_third[:].rearrange("p v d -> p (v d)"), y[HALF][:], ACT.Square, scale=SQ_SCALE)
+        for i in range(2):
+            weigh_and_sum((6 + i) * EIGHTH)
+        for vs in (slice(VQ, VQ + VE), slice(VQ + VE, VH)):
+            nc.vector.tensor_reduce(beam2[:, vs], ys[:, vs, :], AX.X, ALU.add)
+        energy2 = sb.tile([P, VH], F32, name="energy2", tag="apo_then_energy")
         nc.vector.tensor_reduce(energy2[:, :VQ], sq_third[:], AX.X, ALU.add)
         nc.vector.tensor_reduce(energy2[:, VQ:], sq_pairs[:], AX.X, ALU.add)
 
         abs_t = sb.tile([P, M], F32, name="abs_t")
         nc.scalar.activation(abs_t[:], sums_t[:], ACT.Abs)
-        sums1 = ps.tile([P, 2, VH], F32, name="sums1")
+        sums1 = ps.tile([P, 2, VH], F32, name="sums1", tag=f"y{QUARTER}")
         nc.tensor.transpose(sums1[:].rearrange("p s v -> p (s v)"), abs_t[:], ident[:])
         sums1_again = ps.tile([P, 2, VH], F32, name="sums1_again", tag="spread0")
         nc.tensor.transpose(sums1_again[:].rearrange("p s v -> p (s v)"), abs_t[:], ident[:])

@@ -72,10 +72,15 @@ def tile_picked_ydas_log_p_kernel(tc, x_words, x_scales, w1, apo, offs, out):
 
         ident = sb.tile([P, P], F32, name="ident")
         make_identity(nc, ident[:])
+        placed = ctx.enter_context(tc.tile_pool(name="placed", bufs=1))
         apo_dv = [
-            [sb.tile([P, 4, VQ], F32, name=f"apo_dv{c}{g}", tag=f"apo_dv{c}{g}") for g in range(2)] for c in range(2)
+            [
+                placed.tile([P, 4, VQ], F32, name="apo_dv00", offset=768),
+                sb.tile([P, 4, VQ], F32, name="apo_dv01", tag="apo_sq_power"),
+            ],
+            [sb.tile([P, 4, VQ], F32, name=f"apo_dv1{g}") for g in range(2)],
         ]
-        apo_vd2 = sb.tile([P, VH, D], F32, name="apo_vd2", tag="apo_then_energy")
+        apo_vd2 = sb.tile([P, VH, D], F32, name="apo_vd2")
         for g in range(2):
             apo_ps = ps.tile([P, 4, V], F32, name=f"apo_ps{g}", tag=f"spread{g}")
             for i in range(4):
@@ -124,22 +129,30 @@ def tile_picked_ydas_log_p_kernel(tc, x_words, x_scales, w1, apo, offs, out):
 
         y_dv = [y[c * QUARTER][:].rearrange("p (v d) -> p d v", d=D) for c in range(2)]
         stacked = sb.tile([P, D, 2, VH], F32, name="stacked", tag="stacked_then_late")
-        y_sum1 = sb.tile([P, VH], F32, name="y_sum1")
-        y_first = [sb.tile([P, D, VQ], F32, name=f"y_first{c}", tag=("copy_sq_power", "copy1")[c]) for c in range(2)]
-        four = sb.tile([P, 4, VH], F32, name="four")
-        two = sb.tile([P, 2, VH], F32, name="two")
+        y_first = sb.tile([P, D, VH], F32, name="y_first")
         low, high = slice(0, D // 2), slice(D // 2, D)
-        nc.scalar.copy(y_first[0][:], y_dv[0])
+        nc.scalar.copy(y_first[:, :, :VQ], y_dv[0])
         nc.scalar.activation(stacked[:, low, 1, :VQ], y_dv[0][:, low], ACT.Square, scale=SQ_SCALE)
         for g, ds in enumerate((low, high)):
             nc.vector.tensor_tensor(stacked[:, ds, 0, :VQ], y_dv[0][:, ds], apo_dv[0][g][:], ALU.mult)
-        nc.gpsimd.tensor_tensor(four[:, :, :VQ], y_first[0][:, low], y_first[0][:, high], ALU.add)
-        nc.scalar.copy(y_first[1][:], y_dv[1])
-        nc.scalar.activation(stacked[:, high, 1, :VQ], y_first[0][:, high], ACT.Square, scale=SQ_SCALE)
-        for g, ds in enumerate((low, high)):
-            nc.vector.tensor_tensor(stacked[:, ds, 0, VQ:], y_dv[1][:, ds], apo_dv[1][g][:], ALU.mult)
-            nc.scalar.activation(stacked[:, ds, 1, VQ:], y_first[1][:, ds], ACT.Square, scale=SQ_SCALE)
-        nc.gpsimd.tensor_tensor(four[:, :, VQ:], y_first[1][:, low], y_first[1][:, high], ALU.add)
+        nc.scalar.copy(y_first[:, :, VQ:], y_dv[1])
+        nc.scalar.activation(stacked[:, high, 1, :VQ], y_first[:, high, :VQ], ACT.Square, scale=SQ_SCALE)
+        nc.vector.tensor_tensor(stacked[:, low, 0, VQ:], y_dv[1][:, low], apo_dv[1][0][:], ALU.mult)
+        nc.gpsimd.tensor_tensor(stacked[:, high, 0, VQ:], y_first[:, high, VQ:], apo_dv[1][1][:], ALU.mult)
+        for ds in (low, high):
+            nc.scalar.activation(stacked[:, ds, 1, VQ:], y_first[:, ds, VQ:], ACT.Square, scale=SQ_SCALE)
+        y_pairs_t = ps.tile([P, M], F32, name="y_pairs_t", tag="spread0")
+        for i in range(D // 2):
+            nc.tensor.matmul(
+                y_pairs_t[:],
+                y_first[:, 2 * i : 2 * i + 2].rearrange("p e v -> p (e v)"),
+                ident[:],
+                start=(i == 0),
+                stop=(i == D // 2 - 1),
+                is_transpose=True,
+            )
+        y_pairs = sb.tile([P, M], F32, name="y_pairs", tag="pairs_then_abs")
+        nc.scalar.copy(y_pairs[:], y_pairs_t[:])
         sums_t = ps.tile([P, M], F32, name="sums_t")
         for d in range(D):
             nc.tensor.matmul(
@@ -150,21 +163,22 @@ def tile_picked_ydas_log_p_kernel(tc, x_words, x_scales, w1, apo, offs, out):
                 stop=(d == D - 1),
                 is_transpose=True,
             )
-        nc.gpsimd.tensor_tensor(two[:], four[:, :2], four[:, 2:], ALU.add)
-        nc.gpsimd.tensor_tensor(y_sum1[:], two[:, 0], two[:, 1], ALU.add)
 
         sq_third = sb.tile([P, VQ, D], F32, name="sq_third")
-        sq_last = sb.tile([P, 2, VQ, D // 2], F32, name="sq_last", tag="copy_sq_power")
+        sq_last = sb.tile([P, 2, VQ, D // 2], F32, name="sq_last", tag="apo_sq_power")
         sq_pairs = sb.tile([P, VQ, D // 2], F32, name="sq_pairs")
-        second = sb.tile([P, HALF + VH], F32, name="second", tag="apo_dv00")
-        ys = second[:, :HALF].rearrange("p (v d) -> p v d", d=D)
-        y_sum2 = second[:, HALF:]
-        beam2 = sb.tile([P, VH], F32, name="beam2")
+        ys_third = placed.tile([P, VQ, D], F32, name="ys_third", offset=0)
+        ys_pairs = sb.tile([P, VQ, D // 2], F32, name="ys_pairs", tag="pairs_then_energy")
+        last = placed.tile([P, QUARTER + VH], F32, name="last", offset=1024)
+        ys_last = last[:, :QUARTER].rearrange("p (v d) -> p v d", d=D)
+        ys = {HALF: ys_third[:], 6 * EIGHTH: ys_last[:, :VE], 7 * EIGHTH: ys_last[:, VE:]}
+        y_sum2 = last[:, QUARTER:]
+        beam2 = placed.tile([P, VH], F32, name="beam2", offset=0)
 
         def weigh_and_sum(first):
             vs = slice((first - HALF) // D, (first - HALF + widths[first]) // D)
             y_vd = y[first][:].rearrange("p (v d) -> p v d", d=D)
-            nc.vector.tensor_tensor(ys[:, vs, :], y_vd, apo_vd2[:, vs, :], ALU.mult)
+            nc.vector.tensor_tensor(ys[first], y_vd, apo_vd2[:, vs, :], ALU.mult)
             nc.vector.tensor_reduce(y_sum2[:, vs], y_vd, AX.X, ALU.add)
 
         for i in range(2):
@@ -174,37 +188,42 @@ def tile_picked_ydas_log_p_kernel(tc, x_words, x_scales, w1, apo, offs, out):
                 ACT.Square,
                 scale=SQ_SCALE,
             )
-        nc.gpsimd.tensor_tensor(sq_pairs[:], sq_last[:, 0], sq_last[:, 1], ALU.add)
         weigh_and_sum(HALF)
-        nc.vector.tensor_reduce(beam2[:, :VQ], ys[:, :VQ, :], AX.X, ALU.add)
+        nc.gpsimd.tensor_tensor(ys_pairs[:], ys_third[:, :, low], ys_third[:, :, high], ALU.add)
+        nc.gpsimd.tensor_tensor(sq_pairs[:], sq_last[:, 0], sq_last[:, 1], ALU.add)
         nc.scalar.activation(sq_third[:].rearrange("p v d -> p (v d)"), y[HALF][:], ACT.Square, scale=SQ_SCALE)
         for i in range(2):
             weigh_and_sum((6 + i) * EIGHTH)
-        for vs in (slice(VQ, VQ + VE), slice(VQ + VE, VH)):
-            nc.vector.tensor_reduce(beam2[:, vs], ys[:, vs, :], AX.X, ALU.add)
-        energy2 = sb.tile([P, VH], F32, name="energy2", tag="apo_then_energy")
+        nc.vector.tensor_reduce(beam2[:, :VQ], ys_pairs[:], AX.X, ALU.add)
+        nc.vector.tensor_reduce(beam2[:, VQ:], ys_last, AX.X, ALU.add)
+        energy2 = sb.tile([P, VH], F32, name="energy2", tag="pairs_then_energy")
         nc.vector.tensor_reduce(energy2[:, :VQ], sq_third[:], AX.X, ALU.add)
         nc.vector.tensor_reduce(energy2[:, VQ:], sq_pairs[:], AX.X, ALU.add)
 
+        y_sum1 = ps.tile([P, 2, VH], F32, name="y_sum1", tag="spread1")
+        nc.tensor.matmul(y_sum1[:], y_pairs[:], ident[:], start=True, stop=False, is_transpose=True)
+        nc.tensor.matmul(y_sum1[:, ::-1, :], y_pairs[:], ident[:], start=False, stop=True, is_transpose=True)
         abs_t = sb.tile([P, M], F32, name="abs_t")
         nc.scalar.activation(abs_t[:], sums_t[:], ACT.Abs)
         sums1 = ps.tile([P, 2, VH], F32, name="sums1", tag=f"y{QUARTER}")
         nc.tensor.transpose(sums1[:].rearrange("p s v -> p (s v)"), abs_t[:], ident[:])
-        sums1_again = ps.tile([P, 2, VH], F32, name="sums1_again", tag="spread0")
+        sums1_again = ps.tile([P, 2, VH], F32, name="sums1_again", tag="y0")
         nc.tensor.transpose(sums1_again[:].rearrange("p s v -> p (s v)"), abs_t[:], ident[:])
 
-        late = sb.tile([P, 2 * V + VH], F32, name="late", tag="stacked_then_late")
-        sum_sq, ln_den, beam2_abs = late[:, :V], late[:, V : 2 * V], late[:, 2 * V :]
-        nc.scalar.activation(sum_sq[:, VH:], y_sum2, ACT.Square)
-        nc.scalar.activation(sum_sq[:, :VH], y_sum1[:], ACT.Square)
-        nc.scalar.activation(beam2_abs, beam2[:], ACT.Abs)
+        late = sb.tile([P, V + VH], F32, name="late", tag="stacked_then_late")
+        ln_den, sum_sq2 = late[:, :V], late[:, V:]
+        sum_sq1 = sb.tile([P, VH], F32, name="sum_sq1")
+        beam2_abs = sb.tile([P, VH], F32, name="beam2_abs", tag="pairs_then_abs")
+        nc.scalar.activation(sum_sq2, y_sum2, ACT.Square)
+        nc.scalar.activation(sum_sq1[:], y_sum1[:, 0, :], ACT.Square)
+        nc.scalar.activation(beam2_abs[:], beam2[:], ACT.Abs)
         nc.scalar.activation(ln_den[:, VH:], energy2[:], ACT.Ln, bias=0.1 * LN_SHIFT, scale=20.0 * LN_SHIFT)
         nc.scalar.activation(ln_den[:, :VH], sums1_again[:, 1, :], ACT.Ln, bias=0.1 * LN_SHIFT, scale=20.0 * LN_SHIFT)
 
-        power = sb.tile([P, V], F32, name="power", tag="copy_sq_power")
+        power = sb.tile([P, V], F32, name="power", tag="apo_sq_power")
         num = sb.tile([P, V], F32, name="num")
-        nc.vector.tensor_tensor(power[:, :VH], sums1[:, 0, :], sum_sq[:, :VH], ALU.mult)
-        nc.vector.tensor_tensor(power[:, VH:], beam2_abs, sum_sq[:, VH:], ALU.mult)
+        nc.vector.tensor_tensor(power[:, :VH], sums1[:, 0, :], sum_sq1[:], ALU.mult)
+        nc.vector.tensor_tensor(power[:, VH:], beam2_abs[:], sum_sq2, ALU.mult)
         nc.vector.tensor_tensor(num[:, :VH], sums1[:, 1, :], power[:, :VH], ALU.add)
         nc.vector.tensor_tensor(num[:, VH:], energy2[:], power[:, VH:], ALU.add)
         ln_num = sb.tile([P, V], F32, name="ln_num")

@@ -13,6 +13,8 @@ QUARTER = S // 4
 VQ = V // 4
 EIGHTH = S // 8
 VE = V // 8
+WARM = 256
+TABLE0, THIRD, SQUARES = 0, 4096, 8192
 FLOPS = 2 * K * M * S
 BYTES = K * T + K // 32 * T + K * M * 4 + S * 4 + P * S // 16 * 2 + M * V * 4
 
@@ -50,12 +52,13 @@ def tile_picked_ydas_log_p_kernel(tc, x_words, x_scales, w1, apo, offs, out):
             w_raw[:].rearrange("p o t m -> p o (t m)"), w1.rearrange("(o p t) m -> p o (t m)", o=PASSES, t=4)
         )
         nc.sync.dma_start(offsets[:], offs)
-        nc.sync.dma_start(apo_vd[:], apo[0:1, :].rearrange("o (v d) -> (o v) d", d=D))
+        nc.scalar.dma_start(apo_vd[:], apo[0:1, :].rearrange("o (v d) -> (o v) d", d=D))
         nc.sync.dma_start(
             scale_table[:].bitcast(I32)[0:P:4, :],
             x_scales.bitcast(I32).rearrange("o q c -> q o c"),
         )
-        word_tables = [sb.tile([P, T], I32, name=f"word_table{o}") for o in range(PASSES)]
+        placed = ctx.enter_context(tc.tile_pool(name="placed", bufs=1))
+        word_tables = [placed.tile([P, T], I32, name="word_table0", offset=TABLE0), sb.tile([P, T], I32, name="word_table1")]
         for o in range(PASSES):
             nc.sync.dma_start(word_tables[o][:], x_words[o].rearrange("p c r -> p (c r)").bitcast(I32))
 
@@ -70,26 +73,6 @@ def tile_picked_ydas_log_p_kernel(tc, x_words, x_scales, w1, apo, offs, out):
         ln_warm = sb.tile([P, 1], F32, name="ln_warm")
         nc.scalar.activation(ln_warm[:], apo_vd[:, 0:1], ACT.Ln, bias=1.0, scale=0.0)
 
-        ident = sb.tile([P, P], F32, name="ident")
-        make_identity(nc, ident[:])
-        placed = ctx.enter_context(tc.tile_pool(name="placed", bufs=1))
-        apo_dv = [
-            [
-                placed.tile([P, 4, VQ], F32, name="apo_dv00", offset=768),
-                sb.tile([P, 4, VQ], F32, name="apo_dv01", tag="apo_sq_power"),
-            ],
-            [sb.tile([P, 4, VQ], F32, name=f"apo_dv1{g}") for g in range(2)],
-        ]
-        apo_vd2 = sb.tile([P, VH, D], F32, name="apo_vd2")
-        for g in range(2):
-            apo_ps = ps.tile([P, 4, V], F32, name=f"apo_ps{g}", tag=f"spread{g}")
-            for i in range(4):
-                d = 4 * g + i
-                nc.tensor.transpose(apo_ps[:, i, :], apo_vd[:, d : d + 1].to_broadcast([P, P]), ident[:])
-            for c in range(2):
-                nc.scalar.copy(apo_dv[c][g][:], apo_ps[:, :, c * VQ : (c + 1) * VQ])
-            nc.scalar.copy(apo_vd2[:, :, 4 * g : 4 * g + 4], apo_ps[:, :, VH:].rearrange("p d v -> p v d"))
-
         picked_scales = sb.tile([P, S], U8, name="picked_scales", align_bytes=64)
         nc.vector.tensor_copy(picked_scales[:], scale_table[:].indirect(offsets[:]))
         for q in (0, 2, 1, 3):
@@ -100,6 +83,36 @@ def tile_picked_ydas_log_p_kernel(tc, x_words, x_scales, w1, apo, offs, out):
 
         picked0 = sb.tile([P, S], U32, name="picked0", tag="scales_then_words", align_bytes=64)
         nc.vector.tensor_copy(picked0[:], word_tables[0][:].bitcast(U32).indirect(offsets[:]))
+
+        ident = sb.tile([P, P], F32, name="ident")
+        make_identity(nc, ident[:])
+        apo_dv = [
+            [
+                placed.tile([P, 4, VQ], F32, name="apo_dv00", offset=THIRD + 768),
+                placed.tile([P, 4, VQ], F32, name="apo_dv01", offset=SQUARES),
+            ],
+            [placed.tile([P, 4, VQ], F32, name=f"apo_dv1{g}", offset=TABLE0 + 512 * g) for g in range(2)],
+        ]
+        apo_vd2 = placed.tile([P, VH, D], F32, name="apo_vd2", offset=TABLE0 + 1024)
+        for g in range(2):
+            apo_ps = ps.tile([P, 4, V], F32, name=f"apo_ps{g}", tag=f"spread{g}")
+            for i in range(4):
+                d = 4 * g + i
+                nc.tensor.transpose(apo_ps[:, i, :], apo_vd[:, d : d + 1].to_broadcast([P, P]), ident[:])
+            for c in range(2):
+                nc.scalar.copy(apo_dv[c][g][:], apo_ps[:, :, c * VQ : (c + 1) * VQ])
+            nc.scalar.copy(apo_vd2[:, :, 4 * g : 4 * g + 4], apo_ps[:, :, VH:].rearrange("p d v -> p v d"))
+
+        warm = ps.tile([P, WARM], F32, name="warm", tag="spread1")
+        nc.tensor.matmul_mx(
+            out=warm[:],
+            lhsT=w_codes[:, :M].bitcast(FP8X4),
+            lhsT_scale=w_plane[:, :M],
+            rhs=picked0[:, :WARM].bitcast(FP8X4),
+            rhs_scale=picked_scales[:, :WARM],
+            start=True,
+            stop=True,
+        )
 
         widths = {0: QUARTER, QUARTER: QUARTER, HALF: QUARTER, 6 * EIGHTH: EIGHTH, 7 * EIGHTH: EIGHTH}
         y = {first: ps.tile([P, n], F32, name=f"y{first}", tag=f"y{first}") for first, n in widths.items()}
@@ -165,15 +178,15 @@ def tile_picked_ydas_log_p_kernel(tc, x_words, x_scales, w1, apo, offs, out):
             )
 
         sq_third = sb.tile([P, VQ, D], F32, name="sq_third")
-        sq_last = sb.tile([P, 2, VQ, D // 2], F32, name="sq_last", tag="apo_sq_power")
+        sq_last = placed.tile([P, 2, VQ, D // 2], F32, name="sq_last", offset=SQUARES)
         sq_pairs = sb.tile([P, VQ, D // 2], F32, name="sq_pairs")
-        ys_third = placed.tile([P, VQ, D], F32, name="ys_third", offset=0)
+        ys_third = placed.tile([P, VQ, D], F32, name="ys_third", offset=THIRD)
         ys_pairs = sb.tile([P, VQ, D // 2], F32, name="ys_pairs", tag="pairs_then_energy")
-        last = placed.tile([P, QUARTER + VH], F32, name="last", offset=1024)
+        last = placed.tile([P, QUARTER + VH], F32, name="last", offset=THIRD + 1024)
         ys_last = last[:, :QUARTER].rearrange("p (v d) -> p v d", d=D)
         ys = {HALF: ys_third[:], 6 * EIGHTH: ys_last[:, :VE], 7 * EIGHTH: ys_last[:, VE:]}
         y_sum2 = last[:, QUARTER:]
-        beam2 = placed.tile([P, VH], F32, name="beam2", offset=0)
+        beam2 = placed.tile([P, VH], F32, name="beam2", offset=THIRD)
 
         def weigh_and_sum(first):
             vs = slice((first - HALF) // D, (first - HALF + widths[first]) // D)
@@ -220,7 +233,7 @@ def tile_picked_ydas_log_p_kernel(tc, x_words, x_scales, w1, apo, offs, out):
         nc.scalar.activation(ln_den[:, VH:], energy2[:], ACT.Ln, bias=0.1 * LN_SHIFT, scale=20.0 * LN_SHIFT)
         nc.scalar.activation(ln_den[:, :VH], sums1_again[:, 1, :], ACT.Ln, bias=0.1 * LN_SHIFT, scale=20.0 * LN_SHIFT)
 
-        power = sb.tile([P, V], F32, name="power", tag="apo_sq_power")
+        power = placed.tile([P, V], F32, name="power", offset=SQUARES)
         num = sb.tile([P, V], F32, name="num")
         nc.vector.tensor_tensor(power[:, :VH], sums1[:, 0, :], sum_sq1[:], ALU.mult)
         nc.vector.tensor_tensor(power[:, VH:], beam2_abs[:], sum_sq2, ALU.mult)

@@ -13,7 +13,6 @@ QUARTER = S // 4
 VQ = V // 4
 EIGHTH = S // 8
 VE = V // 8
-WARM = 256
 TABLE0, THIRD, SQUARES = 0, 4096, 8192
 FLOPS = 2 * K * M * S
 BYTES = K * T + K // 32 * T + K * M * 4 + S * 4 + P * S // 16 * 2 + M * V * 4
@@ -103,13 +102,13 @@ def tile_picked_ydas_log_p_kernel(tc, x_words, x_scales, w1, apo, offs, out):
                 nc.scalar.copy(apo_dv[c][g][:], apo_ps[:, :, c * VQ : (c + 1) * VQ])
             nc.scalar.copy(apo_vd2[:, :, 4 * g : 4 * g + 4], apo_ps[:, :, VH:].rearrange("p d v -> p v d"))
 
-        warm = ps.tile([P, WARM], F32, name="warm", tag="spread1")
+        warm = ps.tile([P, PASSES * M], F32, name="warm", tag="spread1")
         nc.tensor.matmul_mx(
             out=warm[:],
             lhsT=w_codes[:, :M].bitcast(FP8X4),
             lhsT_scale=w_plane[:, :M],
-            rhs=picked0[:, :WARM].bitcast(FP8X4),
-            rhs_scale=picked_scales[:, :WARM],
+            rhs=w_codes[:].bitcast(FP8X4),
+            rhs_scale=w_plane[:],
             start=True,
             stop=True,
         )

@@ -102,13 +102,13 @@ def tile_picked_ydas_log_p_kernel(tc, x_words, x_scales, w1, apo, offs, out):
                 nc.scalar.copy(apo_dv[c][g][:], apo_ps[:, :, c * VQ : (c + 1) * VQ])
             nc.scalar.copy(apo_vd2[:, :, 4 * g : 4 * g + 4], apo_ps[:, :, VH:].rearrange("p d v -> p v d"))
 
-        warm = ps.tile([P, PASSES * M], F32, name="warm", tag="spread1")
+        warm = ps.tile([P, M], F32, name="warm", tag="spread1")
         nc.tensor.matmul_mx(
             out=warm[:],
             lhsT=w_codes[:, :M].bitcast(FP8X4),
             lhsT_scale=w_plane[:, :M],
-            rhs=w_codes[:].bitcast(FP8X4),
-            rhs_scale=w_plane[:],
+            rhs=w_codes[:, M:].bitcast(FP8X4),
+            rhs_scale=w_plane[:, M:],
             start=True,
             stop=True,
         )

@@ -13,7 +13,6 @@ QUARTER = S // 4
 VQ = V // 4
 EIGHTH = S // 8
 VE = V // 8
-TABLE0, THIRD, SQUARES = 0, 4096, 8192
 FLOPS = 2 * K * M * S
 BYTES = K * T + K // 32 * T + K * M * 4 + S * 4 + P * S // 16 * 2 + M * V * 4
 
@@ -40,13 +39,13 @@ def tile_picked_ydas_log_p_kernel(tc, x_words, x_scales, w1, apo, offs, out):
         offsets = sb.tile([P, S // 16], U16, name="offsets")
         apo_vd = sb.tile([P, D], F32, name="apo_vd")
 
-        scale_table = sb.tile([P, T], U8, name="scale_table", tag="scales_then_words", align_bytes=64)
+        scale_table = sb.tile([P, T], U8, name="scale_table", tag="scales_then_words", align_bytes=256)
         nc.gpsimd.memset(scale_table[:].bitcast(I32)[:, : T // 8], 0)
         nc.vector.memset(scale_table[:].bitcast(I32)[:, T // 8 :], 0)
-        x_planes = sb.tile([P, PASSES * S], U8, name="x_planes", align_bytes=64)
+        x_planes = sb.tile([P, PASSES * S], U8, name="x_planes", align_bytes=256)
         nc.vector.memset(x_planes[:].bitcast(I32), 0)
 
-        w_raw = sb.tile([P, PASSES, 4, M], F32, name="w_raw")
+        w_raw = sb.tile([P, PASSES, 4, M], F32, name="w_raw", align_bytes=256)
         nc.sync.dma_start(
             w_raw[:].rearrange("p o t m -> p o (t m)"), w1.rearrange("(o p t) m -> p o (t m)", o=PASSES, t=4)
         )
@@ -57,7 +56,10 @@ def tile_picked_ydas_log_p_kernel(tc, x_words, x_scales, w1, apo, offs, out):
             x_scales.bitcast(I32).rearrange("o q c -> q o c"),
         )
         placed = ctx.enter_context(tc.tile_pool(name="placed", bufs=1))
-        word_tables = [placed.tile([P, T], I32, name="word_table0", offset=TABLE0), sb.tile([P, T], I32, name="word_table1")]
+        word_tables = [
+            placed.tile([P, T], I32, name="word_table0", offset=0, align_bytes=256),
+            sb.tile([P, T], I32, name="word_table1", align_bytes=256),
+        ]
         for o in range(PASSES):
             nc.sync.dma_start(word_tables[o][:], x_words[o].rearrange("p c r -> p (c r)").bitcast(I32))
 
@@ -69,8 +71,10 @@ def tile_picked_ydas_log_p_kernel(tc, x_words, x_scales, w1, apo, offs, out):
             out=w_codes[:].bitcast(FP8X4), scales=w_plane[:], in_=w_grouped[:].rearrange("p o m t -> p (o m t)")
         )
 
+        ones = sb.tile([P, 1], F32, name="ones")
+        nc.gpsimd.memset(ones[:], 1.0)
         ln_warm = sb.tile([P, 1], F32, name="ln_warm")
-        nc.scalar.activation(ln_warm[:], apo_vd[:, 0:1], ACT.Ln, bias=1.0, scale=0.0)
+        nc.scalar.activation(ln_warm[:], ones[:], ACT.Ln)
 
         picked_scales = sb.tile([P, S], U8, name="picked_scales", align_bytes=64)
         nc.vector.tensor_copy(picked_scales[:], scale_table[:].indirect(offsets[:]))
@@ -80,26 +84,24 @@ def tile_picked_ydas_log_p_kernel(tc, x_words, x_scales, w1, apo, offs, out):
                 picked_scales[:].bitcast(I32)[32 * q : 32 * q + 32 : 4, :],
             )
 
-        picked0 = sb.tile([P, S], U32, name="picked0", tag="scales_then_words", align_bytes=64)
+        picked0 = sb.tile([P, S], U32, name="picked0", tag="scales_then_words", align_bytes=256)
         nc.vector.tensor_copy(picked0[:], word_tables[0][:].bitcast(U32).indirect(offsets[:]))
 
         ident = sb.tile([P, P], F32, name="ident")
         make_identity(nc, ident[:])
-        apo_dv = [
-            [
-                placed.tile([P, 4, VQ], F32, name="apo_dv00", offset=THIRD + 768),
-                placed.tile([P, 4, VQ], F32, name="apo_dv01", offset=SQUARES),
-            ],
-            [placed.tile([P, 4, VQ], F32, name=f"apo_dv1{g}", offset=TABLE0 + 512 * g) for g in range(2)],
+        apo_first = placed.tile([P, D, VQ], F32, name="apo_first", offset=0)
+        apo_second = [
+            placed.tile([P, D // 2, VQ], F32, name="apo_second0", offset=1024),
+            placed.tile([P, D // 2, VQ], F32, name="apo_second1", offset=1536),
         ]
-        apo_vd2 = placed.tile([P, VH, D], F32, name="apo_vd2", offset=TABLE0 + 1024)
+        apo_vd2 = placed.tile([P, VH, D], F32, name="apo_vd2", offset=2048)
         for g in range(2):
             apo_ps = ps.tile([P, 4, V], F32, name=f"apo_ps{g}", tag=f"spread{g}")
             for i in range(4):
                 d = 4 * g + i
                 nc.tensor.transpose(apo_ps[:, i, :], apo_vd[:, d : d + 1].to_broadcast([P, P]), ident[:])
-            for c in range(2):
-                nc.scalar.copy(apo_dv[c][g][:], apo_ps[:, :, c * VQ : (c + 1) * VQ])
+            nc.scalar.copy(apo_first[:, 4 * g : 4 * g + 4, :], apo_ps[:, :, :VQ])
+            nc.scalar.copy(apo_second[g][:], apo_ps[:, :, VQ:VH])
             nc.scalar.copy(apo_vd2[:, :, 4 * g : 4 * g + 4], apo_ps[:, :, VH:].rearrange("p d v -> p v d"))
 
         warm = ps.tile([P, M], F32, name="warm", tag="spread1")
@@ -113,7 +115,7 @@ def tile_picked_ydas_log_p_kernel(tc, x_words, x_scales, w1, apo, offs, out):
             stop=True,
         )
 
-        widths = {0: QUARTER, QUARTER: QUARTER, HALF: QUARTER, 6 * EIGHTH: EIGHTH, 7 * EIGHTH: EIGHTH}
+        widths = {c * QUARTER: QUARTER for c in range(4)}
         y = {first: ps.tile([P, n], F32, name=f"y{first}", tag=f"y{first}") for first, n in widths.items()}
         picked1 = sb.tile([P, S], U32, name="picked1", align_bytes=64)
 
@@ -139,100 +141,92 @@ def tile_picked_ydas_log_p_kernel(tc, x_words, x_scales, w1, apo, offs, out):
                     if first // QUARTER == c:
                         product(first, o, picked)
 
-        y_dv = [y[c * QUARTER][:].rearrange("p (v d) -> p d v", d=D) for c in range(2)]
+        def foci(first):
+            return slice(first // D, (first + widths[first]) // D)
+
+        def foci2(first):
+            return slice((first - HALF) // D, (first - HALF + widths[first]) // D)
+
+        def y_dv(first):
+            return y[first][:].rearrange("p (v d) -> p d v", d=D)
+
+        def y_vd(first):
+            return y[first][:].rearrange("p (v d) -> p v d", d=D)
+
+        def add_transposed(bank, tiles):
+            for i, tile in enumerate(tiles):
+                nc.tensor.matmul(bank, tile, ident[:], start=(i == 0), stop=(i == len(tiles) - 1), is_transpose=True)
+
+        def back_doubled(bank, pairs):
+            nc.tensor.matmul(bank, pairs, ident[:], start=True, stop=False, is_transpose=True)
+            nc.tensor.matmul(bank[:, ::-1, :], pairs, ident[:], start=False, stop=True, is_transpose=True)
+
         stacked = sb.tile([P, D, 2, VH], F32, name="stacked", tag="stacked_then_late")
         y_first = sb.tile([P, D, VH], F32, name="y_first")
+        ys2 = sb.tile([P, VH, D], F32, name="ys2")
+        y_sum2 = sb.tile([P, VH], F32, name="y_sum2")
         low, high = slice(0, D // 2), slice(D // 2, D)
-        nc.scalar.copy(y_first[:, :, :VQ], y_dv[0])
-        nc.scalar.activation(stacked[:, low, 1, :VQ], y_dv[0][:, low], ACT.Square, scale=SQ_SCALE)
-        for g, ds in enumerate((low, high)):
-            nc.vector.tensor_tensor(stacked[:, ds, 0, :VQ], y_dv[0][:, ds], apo_dv[0][g][:], ALU.mult)
-        nc.scalar.copy(y_first[:, :, VQ:], y_dv[1])
-        nc.scalar.activation(stacked[:, high, 1, :VQ], y_first[:, high, :VQ], ACT.Square, scale=SQ_SCALE)
-        nc.vector.tensor_tensor(stacked[:, low, 0, VQ:], y_dv[1][:, low], apo_dv[1][0][:], ALU.mult)
-        nc.gpsimd.tensor_tensor(stacked[:, high, 0, VQ:], y_first[:, high, VQ:], apo_dv[1][1][:], ALU.mult)
-        for ds in (low, high):
-            nc.scalar.activation(stacked[:, ds, 1, VQ:], y_first[:, ds, VQ:], ACT.Square, scale=SQ_SCALE)
-        y_pairs_t = ps.tile([P, M], F32, name="y_pairs_t", tag="spread0")
-        for i in range(D // 2):
-            nc.tensor.matmul(
-                y_pairs_t[:],
-                y_first[:, 2 * i : 2 * i + 2].rearrange("p e v -> p (e v)"),
-                ident[:],
-                start=(i == 0),
-                stop=(i == D // 2 - 1),
-                is_transpose=True,
+
+        for first, parts in ((0, [(slice(0, D), apo_first)]), (QUARTER, list(zip((low, high), apo_second)))):
+            vs = foci(first)
+            nc.scalar.copy(y_first[:, :, vs], y_dv(first))
+            for ds, weights in parts:
+                nc.scalar.activation(stacked[:, ds, 1, vs], y_dv(first)[:, ds], ACT.Square, scale=SQ_SCALE)
+                nc.gpsimd.tensor_tensor(stacked[:, ds, 0, vs], y_first[:, ds, vs], weights[:], ALU.mult)
+
+        sq2 = sb.tile([P, 2, 2, VQ, D // 2], F32, name="sq2")
+        sq_pairs = sb.tile([P, 2, VQ, D // 2], F32, name="sq_pairs")
+        beam2 = sb.tile([P, VH], F32, name="beam2", tag="beam_then_ln")
+        energy2 = sb.tile([P, VH], F32, name="energy2")
+
+        def square(c):
+            nc.scalar.activation(
+                sq2[:, c], y[HALF + c * QUARTER][:].rearrange("p (v u e) -> p u v e", u=2, e=D // 2), ACT.Square, scale=SQ_SCALE
             )
+
+        def weigh_and_sum(c):
+            first = HALF + c * QUARTER
+            vs = foci2(first)
+            nc.vector.tensor_tensor(ys2[:, vs], y_vd(first), apo_vd2[:, vs, :], ALU.mult)
+            nc.vector.tensor_reduce(y_sum2[:, vs], y_vd(first), AX.X, ALU.add)
+            nc.vector.tensor_reduce(beam2[:, vs], ys2[:, vs], AX.X, ALU.add)
+
+        square(1)
+        weigh_and_sum(0)
+        square(0)
+        weigh_and_sum(1)
+        y_pairs_t = ps.tile([P, M], F32, name="y_pairs_t", tag="spread0")
+        add_transposed(y_pairs_t[:], [y_first[:, 2 * i : 2 * i + 2].rearrange("p e v -> p (e v)") for i in range(D // 2)])
         y_pairs = sb.tile([P, M], F32, name="y_pairs", tag="pairs_then_abs")
         nc.scalar.copy(y_pairs[:], y_pairs_t[:])
+        for c in (1, 0):
+            nc.gpsimd.tensor_tensor(sq_pairs[:, c], sq2[:, c, 0], sq2[:, c, 1], ALU.add)
+            nc.vector.tensor_reduce(energy2[:, c * VQ : (c + 1) * VQ], sq_pairs[:, c], AX.X, ALU.add)
+
         sums_t = ps.tile([P, M], F32, name="sums_t")
-        for d in range(D):
-            nc.tensor.matmul(
-                sums_t[:],
-                stacked[:, d].rearrange("p s v -> p (s v)"),
-                ident[:],
-                start=(d == 0),
-                stop=(d == D - 1),
-                is_transpose=True,
-            )
-
-        sq_third = sb.tile([P, VQ, D], F32, name="sq_third")
-        sq_last = placed.tile([P, 2, VQ, D // 2], F32, name="sq_last", offset=SQUARES)
-        sq_pairs = sb.tile([P, VQ, D // 2], F32, name="sq_pairs")
-        ys_third = placed.tile([P, VQ, D], F32, name="ys_third", offset=THIRD)
-        ys_pairs = sb.tile([P, VQ, D // 2], F32, name="ys_pairs", tag="pairs_then_energy")
-        last = placed.tile([P, QUARTER + VH], F32, name="last", offset=THIRD + 1024)
-        ys_last = last[:, :QUARTER].rearrange("p (v d) -> p v d", d=D)
-        ys = {HALF: ys_third[:], 6 * EIGHTH: ys_last[:, :VE], 7 * EIGHTH: ys_last[:, VE:]}
-        y_sum2 = last[:, QUARTER:]
-        beam2 = placed.tile([P, VH], F32, name="beam2", offset=THIRD)
-
-        def weigh_and_sum(first):
-            vs = slice((first - HALF) // D, (first - HALF + widths[first]) // D)
-            y_vd = y[first][:].rearrange("p (v d) -> p v d", d=D)
-            nc.vector.tensor_tensor(ys[first], y_vd, apo_vd2[:, vs, :], ALU.mult)
-            nc.vector.tensor_reduce(y_sum2[:, vs], y_vd, AX.X, ALU.add)
-
-        for i in range(2):
-            nc.scalar.activation(
-                sq_last[:, :, i * VE : (i + 1) * VE],
-                y[(6 + i) * EIGHTH][:].rearrange("p (v u e) -> p u v e", u=2, e=D // 2),
-                ACT.Square,
-                scale=SQ_SCALE,
-            )
-        weigh_and_sum(HALF)
-        nc.gpsimd.tensor_tensor(ys_pairs[:], ys_third[:, :, low], ys_third[:, :, high], ALU.add)
-        nc.gpsimd.tensor_tensor(sq_pairs[:], sq_last[:, 0], sq_last[:, 1], ALU.add)
-        nc.scalar.activation(sq_third[:].rearrange("p v d -> p (v d)"), y[HALF][:], ACT.Square, scale=SQ_SCALE)
-        for i in range(2):
-            weigh_and_sum((6 + i) * EIGHTH)
-        nc.vector.tensor_reduce(beam2[:, :VQ], ys_pairs[:], AX.X, ALU.add)
-        nc.vector.tensor_reduce(beam2[:, VQ:], ys_last, AX.X, ALU.add)
-        energy2 = sb.tile([P, VH], F32, name="energy2", tag="pairs_then_energy")
-        nc.vector.tensor_reduce(energy2[:, :VQ], sq_third[:], AX.X, ALU.add)
-        nc.vector.tensor_reduce(energy2[:, VQ:], sq_pairs[:], AX.X, ALU.add)
+        add_transposed(sums_t[:], [stacked[:, d].rearrange("p s v -> p (s v)") for d in range(D)])
+        abs_t = sb.tile([P, M], F32, name="abs_t", tag="abs_then_power")
+        nc.scalar.activation(abs_t[:], sums_t[:], ACT.Abs)
 
         y_sum1 = ps.tile([P, 2, VH], F32, name="y_sum1", tag="spread1")
-        nc.tensor.matmul(y_sum1[:], y_pairs[:], ident[:], start=True, stop=False, is_transpose=True)
-        nc.tensor.matmul(y_sum1[:, ::-1, :], y_pairs[:], ident[:], start=False, stop=True, is_transpose=True)
-        abs_t = sb.tile([P, M], F32, name="abs_t")
-        nc.scalar.activation(abs_t[:], sums_t[:], ACT.Abs)
+        back_doubled(y_sum1[:], y_pairs[:])
         sums1 = ps.tile([P, 2, VH], F32, name="sums1", tag=f"y{QUARTER}")
         nc.tensor.transpose(sums1[:].rearrange("p s v -> p (s v)"), abs_t[:], ident[:])
         sums1_again = ps.tile([P, 2, VH], F32, name="sums1_again", tag="y0")
         nc.tensor.transpose(sums1_again[:].rearrange("p s v -> p (s v)"), abs_t[:], ident[:])
 
-        late = sb.tile([P, V + VH], F32, name="late", tag="stacked_then_late")
-        ln_den, sum_sq2 = late[:, :V], late[:, V:]
-        sum_sq1 = sb.tile([P, VH], F32, name="sum_sq1")
+        late = sb.tile([P, V], F32, name="late", tag="stacked_then_late")
+        ln_den1, sum_sq2 = late[:, :VH], late[:, VH:]
         beam2_abs = sb.tile([P, VH], F32, name="beam2_abs", tag="pairs_then_abs")
-        nc.scalar.activation(sum_sq2, y_sum2, ACT.Square)
+        sum_sq1 = sb.tile([P, VH], F32, name="sum_sq1")
+        nc.scalar.activation(sum_sq2, y_sum2[:], ACT.Square)
         nc.scalar.activation(sum_sq1[:], y_sum1[:, 0, :], ACT.Square)
         nc.scalar.activation(beam2_abs[:], beam2[:], ACT.Abs)
-        nc.scalar.activation(ln_den[:, VH:], energy2[:], ACT.Ln, bias=0.1 * LN_SHIFT, scale=20.0 * LN_SHIFT)
-        nc.scalar.activation(ln_den[:, :VH], sums1_again[:, 1, :], ACT.Ln, bias=0.1 * LN_SHIFT, scale=20.0 * LN_SHIFT)
+        ln_den2 = sb.tile([P, VH], F32, name="ln_den2", tag="beam_then_ln")
+        nc.scalar.activation(ln_den2[:], energy2[:], ACT.Ln, bias=0.1 * LN_SHIFT, scale=20.0 * LN_SHIFT)
+        nc.scalar.activation(ln_den1, sums1_again[:, 1, :], ACT.Ln, bias=0.1 * LN_SHIFT, scale=20.0 * LN_SHIFT)
 
-        power = placed.tile([P, V], F32, name="power", offset=SQUARES)
+        power = sb.tile([P, V], F32, name="power", tag="abs_then_power")
         num = sb.tile([P, V], F32, name="num")
         nc.vector.tensor_tensor(power[:, :VH], sums1[:, 0, :], sum_sq1[:], ALU.mult)
         nc.vector.tensor_tensor(power[:, VH:], beam2_abs[:], sum_sq2, ALU.mult)
@@ -240,7 +234,7 @@ def tile_picked_ydas_log_p_kernel(tc, x_words, x_scales, w1, apo, offs, out):
         nc.vector.tensor_tensor(num[:, VH:], energy2[:], power[:, VH:], ALU.add)
         ln_num = sb.tile([P, V], F32, name="ln_num")
         result = sb.tile([P, V], F32, name="result")
-        for vs in (slice(0, VH), slice(VH, V)):
+        for vs, ln_den in ((slice(0, VH), ln_den1), (slice(VH, V), ln_den2[:])):
             nc.scalar.activation(ln_num[:, vs], num[:, vs], ACT.Ln, bias=0.005 * LN_SHIFT, scale=LN_SHIFT)
-            nc.vector.tensor_tensor(result[:, vs], ln_num[:, vs], ln_den[:, vs], ALU.subtract)
+            nc.vector.tensor_tensor(result[:, vs], ln_num[:, vs], ln_den, ALU.subtract)
         nc.sync.dma_start(out, result[:])

@@ -13,6 +13,7 @@ QUARTER = S // 4
 VQ = V // 4
 EIGHTH = S // 8
 VE = V // 8
+HELD = 16384
 FLOPS = 2 * K * M * S
 BYTES = K * T + K // 32 * T + K * M * 4 + S * 4 + P * S // 16 * 2 + M * V * 4
 
@@ -76,6 +77,9 @@ def tile_picked_ydas_log_p_kernel(tc, x_words, x_scales, w1, apo, offs, out):
         ln_warm = sb.tile([P, 1], F32, name="ln_warm")
         nc.scalar.activation(ln_warm[:], ones[:], ACT.Ln)
 
+        sq_scale = placed.tile([P, 1], F32, name="sq_scale", offset=HELD)
+        nc.gpsimd.tensor_scalar(sq_scale[:], ones[:], SQ_SCALE, 0.0, ALU.mult, ALU.add)
+
         picked_scales = sb.tile([P, S], U8, name="picked_scales", align_bytes=64)
         nc.vector.tensor_copy(picked_scales[:], scale_table[:].indirect(offsets[:]))
         for q in (0, 2, 1, 3):
@@ -89,19 +93,14 @@ def tile_picked_ydas_log_p_kernel(tc, x_words, x_scales, w1, apo, offs, out):
 
         ident = sb.tile([P, P], F32, name="ident")
         make_identity(nc, ident[:])
-        apo_first = placed.tile([P, D, VQ], F32, name="apo_first", offset=0)
-        apo_second = [
-            placed.tile([P, D // 2, VQ], F32, name="apo_second0", offset=1024),
-            placed.tile([P, D // 2, VQ], F32, name="apo_second1", offset=1536),
-        ]
+        apo_dv = placed.tile([P, D, VH], F32, name="apo_dv", offset=0)
         apo_vd2 = placed.tile([P, VH, D], F32, name="apo_vd2", offset=2048)
         for g in range(2):
             apo_ps = ps.tile([P, 4, V], F32, name=f"apo_ps{g}", tag=f"spread{g}")
             for i in range(4):
                 d = 4 * g + i
                 nc.tensor.transpose(apo_ps[:, i, :], apo_vd[:, d : d + 1].to_broadcast([P, P]), ident[:])
-            nc.scalar.copy(apo_first[:, 4 * g : 4 * g + 4, :], apo_ps[:, :, :VQ])
-            nc.scalar.copy(apo_second[g][:], apo_ps[:, :, VQ:VH])
+            nc.scalar.copy(apo_dv[:, 4 * g : 4 * g + 4, :], apo_ps[:, :, :VH])
             nc.scalar.copy(apo_vd2[:, :, 4 * g : 4 * g + 4], apo_ps[:, :, VH:].rearrange("p d v -> p v d"))
 
         warm = ps.tile([P, M], F32, name="warm", tag="spread1")
@@ -115,7 +114,7 @@ def tile_picked_ydas_log_p_kernel(tc, x_words, x_scales, w1, apo, offs, out):
             stop=True,
         )
 
-        widths = {c * QUARTER: QUARTER for c in range(4)}
+        widths = {0: QUARTER, 2 * EIGHTH: EIGHTH, 3 * EIGHTH: EIGHTH, HALF: QUARTER, 6 * EIGHTH: EIGHTH, 7 * EIGHTH: EIGHTH}
         y = {first: ps.tile([P, n], F32, name=f"y{first}", tag=f"y{first}") for first, n in widths.items()}
         picked1 = sb.tile([P, S], U32, name="picked1", align_bytes=64)
 
@@ -163,70 +162,87 @@ def tile_picked_ydas_log_p_kernel(tc, x_words, x_scales, w1, apo, offs, out):
 
         stacked = sb.tile([P, D, 2, VH], F32, name="stacked", tag="stacked_then_late")
         y_first = sb.tile([P, D, VH], F32, name="y_first")
-        ys2 = sb.tile([P, VH, D], F32, name="ys2")
-        y_sum2 = sb.tile([P, VH], F32, name="y_sum2")
         low, high = slice(0, D // 2), slice(D // 2, D)
+        first_quarter, third_eighth, fourth_eighth = foci(0), foci(2 * EIGHTH), foci(3 * EIGHTH)
 
-        for first, parts in ((0, [(slice(0, D), apo_first)]), (QUARTER, list(zip((low, high), apo_second)))):
-            vs = foci(first)
-            nc.scalar.copy(y_first[:, :, vs], y_dv(first))
-            for ds, weights in parts:
-                nc.scalar.activation(stacked[:, ds, 1, vs], y_dv(first)[:, ds], ACT.Square, scale=SQ_SCALE)
-                nc.gpsimd.tensor_tensor(stacked[:, ds, 0, vs], y_first[:, ds, vs], weights[:], ALU.mult)
+        def weigh_copy(ds, vs):
+            nc.gpsimd.tensor_tensor(stacked[:, ds, 0, vs], y_first[:, ds, vs], apo_dv[:, ds, vs], ALU.mult)
 
-        sq2 = sb.tile([P, 2, 2, VQ, D // 2], F32, name="sq2")
-        sq_pairs = sb.tile([P, 2, VQ, D // 2], F32, name="sq_pairs")
-        beam2 = sb.tile([P, VH], F32, name="beam2", tag="beam_then_ln")
-        energy2 = sb.tile([P, VH], F32, name="energy2")
+        nc.scalar.copy(y_first[:, :, first_quarter], y_dv(0))
+        nc.vector.tensor_tensor(stacked[:, low, 0, first_quarter], y_dv(0)[:, low], apo_dv[:, low, first_quarter], ALU.mult)
+        weigh_copy(high, first_quarter)
+        nc.scalar.copy(y_first[:, :, third_eighth], y_dv(2 * EIGHTH))
+        nc.vector.tensor_tensor(stacked[:, :, 0, third_eighth], y_dv(2 * EIGHTH), apo_dv[:, :, third_eighth], ALU.mult)
+        nc.scalar.activation(stacked[:, low, 1, first_quarter], y_first[:, low, first_quarter], ACT.Square, scale=sq_scale[:])
+        nc.scalar.copy(y_first[:, :, fourth_eighth], y_dv(3 * EIGHTH))
+        for ds in (low, high):
+            weigh_copy(ds, fourth_eighth)
+        nc.scalar.activation(stacked[:, high, 1, :VQ], y_first[:, high, :VQ], ACT.Square, scale=SQ_SCALE)
+        nc.scalar.activation(stacked[:, low, 1, VQ:], y_first[:, low, VQ:], ACT.Square, scale=SQ_SCALE)
 
-        def square(c):
+        held = placed.tile([P, 3 * QUARTER + VH], F32, name="held", offset=HELD)
+        ys2 = held[:, :HALF].rearrange("p (v d) -> p v d", d=D)
+        ys_third, ys_last = ys2[:, :VQ], ys2[:, VQ:]
+        sq_last = held[:, HALF : 3 * QUARTER].rearrange("p (u v e) -> p u v e", u=2, e=D // 2)
+        y_sum2 = held[:, 3 * QUARTER :]
+
+        def square_last(i):
             nc.scalar.activation(
-                sq2[:, c], y[HALF + c * QUARTER][:].rearrange("p (v u e) -> p u v e", u=2, e=D // 2), ACT.Square, scale=SQ_SCALE
+                sq_last[:, :, i * VE : (i + 1) * VE],
+                y[(6 + i) * EIGHTH][:].rearrange("p (v u e) -> p u v e", u=2, e=D // 2),
+                ACT.Square,
+                scale=SQ_SCALE,
             )
 
-        def weigh_and_sum(c):
-            first = HALF + c * QUARTER
+        square_last(0)
+        nc.scalar.activation(stacked[:, high, 1, VQ:], y_first[:, high, VQ:], ACT.Square, scale=SQ_SCALE)
+        square_last(1)
+        for first in (HALF, 6 * EIGHTH, 7 * EIGHTH):
             vs = foci2(first)
             nc.vector.tensor_tensor(ys2[:, vs], y_vd(first), apo_vd2[:, vs, :], ALU.mult)
             nc.vector.tensor_reduce(y_sum2[:, vs], y_vd(first), AX.X, ALU.add)
-            nc.vector.tensor_reduce(beam2[:, vs], ys2[:, vs], AX.X, ALU.add)
 
-        square(1)
-        weigh_and_sum(0)
-        square(0)
-        weigh_and_sum(1)
+        sq_third = sb.tile([P, VQ, D], F32, name="sq_third")
+        nc.scalar.activation(sq_third[:].rearrange("p v d -> p (v d)"), y[HALF][:], ACT.Square, scale=SQ_SCALE)
         y_pairs_t = ps.tile([P, M], F32, name="y_pairs_t", tag="spread0")
         add_transposed(y_pairs_t[:], [y_first[:, 2 * i : 2 * i + 2].rearrange("p e v -> p (e v)") for i in range(D // 2)])
         y_pairs = sb.tile([P, M], F32, name="y_pairs", tag="pairs_then_abs")
         nc.scalar.copy(y_pairs[:], y_pairs_t[:])
-        for c in (1, 0):
-            nc.gpsimd.tensor_tensor(sq_pairs[:, c], sq2[:, c, 0], sq2[:, c, 1], ALU.add)
-            nc.vector.tensor_reduce(energy2[:, c * VQ : (c + 1) * VQ], sq_pairs[:, c], AX.X, ALU.add)
+        ys_pairs = sb.tile([P, VQ, D // 2], F32, name="ys_pairs", tag="pairs_then_energy")
+        nc.gpsimd.tensor_tensor(ys_pairs[:], ys_third[:, :, low], ys_third[:, :, high], ALU.add)
+        sq_pairs = sb.tile([P, VQ, D // 2], F32, name="sq_pairs")
+        nc.gpsimd.tensor_tensor(sq_pairs[:], sq_last[:, 0], sq_last[:, 1], ALU.add)
+        beam2 = sb.tile([P, VH], F32, name="beam2", tag="beam_then_ln")
+        nc.vector.tensor_reduce(beam2[:, :VQ], ys_pairs[:], AX.X, ALU.add)
+        nc.vector.tensor_reduce(beam2[:, VQ:], ys_last, AX.X, ALU.add)
+        energy2 = sb.tile([P, VH], F32, name="energy2", tag="pairs_then_energy")
+        nc.vector.tensor_reduce(energy2[:, :VQ], sq_third[:], AX.X, ALU.add)
+        nc.vector.tensor_reduce(energy2[:, VQ:], sq_pairs[:], AX.X, ALU.add)
 
-        sums_t = ps.tile([P, M], F32, name="sums_t")
+        sums_t = ps.tile([P, M], F32, name="sums_t", tag="spread1")
         add_transposed(sums_t[:], [stacked[:, d].rearrange("p s v -> p (s v)") for d in range(D)])
-        abs_t = sb.tile([P, M], F32, name="abs_t", tag="abs_then_power")
+        abs_t = sb.tile([P, M], F32, name="abs_t")
         nc.scalar.activation(abs_t[:], sums_t[:], ACT.Abs)
 
-        y_sum1 = ps.tile([P, 2, VH], F32, name="y_sum1", tag="spread1")
+        y_sum1 = ps.tile([P, 2, VH], F32, name="y_sum1", tag="y0")
         back_doubled(y_sum1[:], y_pairs[:])
-        sums1 = ps.tile([P, 2, VH], F32, name="sums1", tag=f"y{QUARTER}")
+        sums1 = ps.tile([P, 2, VH], F32, name="sums1", tag=f"y{2 * EIGHTH}")
         nc.tensor.transpose(sums1[:].rearrange("p s v -> p (s v)"), abs_t[:], ident[:])
-        sums1_again = ps.tile([P, 2, VH], F32, name="sums1_again", tag="y0")
+        sums1_again = ps.tile([P, 2, VH], F32, name="sums1_again", tag=f"y{3 * EIGHTH}")
         nc.tensor.transpose(sums1_again[:].rearrange("p s v -> p (s v)"), abs_t[:], ident[:])
 
         late = sb.tile([P, V], F32, name="late", tag="stacked_then_late")
         ln_den1, sum_sq2 = late[:, :VH], late[:, VH:]
         beam2_abs = sb.tile([P, VH], F32, name="beam2_abs", tag="pairs_then_abs")
         sum_sq1 = sb.tile([P, VH], F32, name="sum_sq1")
-        nc.scalar.activation(sum_sq2, y_sum2[:], ACT.Square)
+        nc.scalar.activation(sum_sq2, y_sum2, ACT.Square)
         nc.scalar.activation(sum_sq1[:], y_sum1[:, 0, :], ACT.Square)
         nc.scalar.activation(beam2_abs[:], beam2[:], ACT.Abs)
         ln_den2 = sb.tile([P, VH], F32, name="ln_den2", tag="beam_then_ln")
         nc.scalar.activation(ln_den2[:], energy2[:], ACT.Ln, bias=0.1 * LN_SHIFT, scale=20.0 * LN_SHIFT)
         nc.scalar.activation(ln_den1, sums1_again[:, 1, :], ACT.Ln, bias=0.1 * LN_SHIFT, scale=20.0 * LN_SHIFT)
 
-        power = sb.tile([P, V], F32, name="power", tag="abs_then_power")
+        power = sb.tile([P, V], F32, name="power")
         num = sb.tile([P, V], F32, name="num")
         nc.vector.tensor_tensor(power[:, :VH], sums1[:, 0, :], sum_sq1[:], ALU.mult)
         nc.vector.tensor_tensor(power[:, VH:], beam2_abs[:], sum_sq2, ALU.mult)

@@ -169,8 +169,7 @@ def tile_picked_ydas_log_p_kernel(tc, x_words, x_scales, w1, apo, offs, out):
             nc.gpsimd.tensor_tensor(stacked[:, ds, 0, vs], y_first[:, ds, vs], apo_dv[:, ds, vs], ALU.mult)
 
         nc.scalar.copy(y_first[:, :, first_quarter], y_dv(0))
-        nc.vector.tensor_tensor(stacked[:, low, 0, first_quarter], y_dv(0)[:, low], apo_dv[:, low, first_quarter], ALU.mult)
-        weigh_copy(high, first_quarter)
+        weigh_copy(slice(0, D), first_quarter)
         nc.scalar.copy(y_first[:, :, third_eighth], y_dv(2 * EIGHTH))
         nc.vector.tensor_tensor(stacked[:, :, 0, third_eighth], y_dv(2 * EIGHTH), apo_dv[:, :, third_eighth], ALU.mult)
         nc.scalar.activation(stacked[:, low, 1, first_quarter], y_first[:, low, first_quarter], ACT.Square, scale=sq_scale[:])

@@ -169,7 +169,7 @@ def tile_picked_ydas_log_p_kernel(tc, x_words, x_scales, w1, apo, offs, out):
             nc.gpsimd.tensor_tensor(stacked[:, ds, 0, vs], y_first[:, ds, vs], apo_dv[:, ds, vs], ALU.mult)
 
         nc.scalar.copy(y_first[:, :, first_quarter], y_dv(0))
-        weigh_copy(slice(0, D), first_quarter)
+        nc.vector.tensor_tensor(stacked[:, :, 0, first_quarter], y_dv(0), apo_dv[:, :, first_quarter], ALU.mult)
         nc.scalar.copy(y_first[:, :, third_eighth], y_dv(2 * EIGHTH))
         nc.vector.tensor_tensor(stacked[:, :, 0, third_eighth], y_dv(2 * EIGHTH), apo_dv[:, :, third_eighth], ALU.mult)
         nc.scalar.activation(stacked[:, low, 1, first_quarter], y_first[:, low, first_quarter], ACT.Square, scale=sq_scale[:])

from contextlib import ExitStack

import concourse.mybir as mybir
from concourse.masks import make_identity

K, T, S, D, M = 1024, 4096, 1024, 8, 128
P = 128
PASSES = 2
V = S // D
HALF = S // 2
VH = V // 2
QUARTER = S // 4
VQ = V // 4
EIGHTH = S // 8
VE = V // 8
HELD = 16384
FLOPS = 2 * K * M * S
BYTES = K * T + K // 32 * T + K * M * 4 + S * 4 + P * S // 16 * 2 + M * V * 4

F32 = mybir.dt.float32
BF16 = mybir.dt.bfloat16
I32 = mybir.dt.int32
U32 = mybir.dt.uint32
U16 = mybir.dt.uint16
U8 = mybir.dt.uint8
FP8X4 = mybir.dt.float8_e4m3fn_x4
ALU = mybir.AluOpType
ACT = mybir.ActivationFunctionType
AX = mybir.AxisListType
LN_SHIFT = 2.0 ** -32
SQ_SCALE = 0.4 ** 0.5


def tile_picked_ydas_log_p_kernel(tc, x_words, x_scales, w1, apo, offs, out):
    nc = tc.nc
    with ExitStack() as ctx:
        sb = ctx.enter_context(tc.tile_pool(name="sb", bufs=1))
        ps = ctx.enter_context(tc.psum_pool(name="ps", bufs=1))

        offsets = sb.tile([P, S // 16], U16, name="offsets")
        apo_vd = sb.tile([P, D], F32, name="apo_vd")

        scale_table = sb.tile([P, T], U8, name="scale_table", tag="scales_then_words", align_bytes=256)
        nc.gpsimd.memset(scale_table[:].bitcast(I32)[:, : T // 8], 0)
        nc.vector.memset(scale_table[:].bitcast(I32)[:, T // 8 :], 0)
        x_planes = sb.tile([P, PASSES * S], U8, name="x_planes", align_bytes=256)
        nc.vector.memset(x_planes[:].bitcast(I32), 0)

        w_raw = sb.tile([P, PASSES, 4, M], F32, name="w_raw", align_bytes=256)
        nc.sync.dma_start(
            w_raw[:].rearrange("p o t m -> p o (t m)"), w1.rearrange("(o p t) m -> p o (t m)", o=PASSES, t=4)
        )
        nc.sync.dma_start(offsets[:], offs)
        nc.scalar.dma_start(apo_vd[:], apo[0:1, :].rearrange("o (v d) -> (o v) d", d=D))
        nc.sync.dma_start(
            scale_table[:].bitcast(I32)[0:P:4, :],
            x_scales.bitcast(I32).rearrange("o q c -> q o c"),
        )
        placed = ctx.enter_context(tc.tile_pool(name="placed", bufs=1))
        word_tables = [
            placed.tile([P, T], I32, name="word_table0", offset=0, align_bytes=256),
            sb.tile([P, T], I32, name="word_table1", align_bytes=256),
        ]
        for o in range(PASSES):
            nc.sync.dma_start(word_tables[o][:], x_words[o].rearrange("p c r -> p (c r)").bitcast(I32))

        w_grouped = sb.tile([P, PASSES, M, 4], BF16, name="w_grouped", align_bytes=64)
        nc.vector.tensor_copy(w_grouped[:], w_raw[:].rearrange("p o t m -> p o m t"))
        w_codes = sb.tile([P, PASSES * M], U32, name="w_codes", align_bytes=64)
        w_plane = sb.tile([P, PASSES * M], U8, name="w_plane", align_bytes=64)
        nc.vector.quantize_mx(
            out=w_codes[:].bitcast(FP8X4), scales=w_plane[:], in_=w_grouped[:].rearrange("p o m t -> p (o m t)")
        )

        ones = sb.tile([P, 1], F32, name="ones")
        nc.gpsimd.memset(ones[:], 1.0)
        ln_warm = sb.tile([P, 1], F32, name="ln_warm")
        nc.scalar.activation(ln_warm[:], ones[:], ACT.Ln)

        sq_scale = placed.tile([P, 1], F32, name="sq_scale", offset=HELD)
        nc.gpsimd.tensor_scalar(sq_scale[:], ones[:], SQ_SCALE, 0.0, ALU.mult, ALU.add)

        picked_scales = sb.tile([P, S], U8, name="picked_scales", align_bytes=64)
        nc.vector.tensor_copy(picked_scales[:], scale_table[:].indirect(offsets[:]))
        for q in (0, 2, 1, 3):
            nc.sync.dma_start(
                x_planes[:].bitcast(I32)[32 * q : 32 * q + 4, :],
                picked_scales[:].bitcast(I32)[32 * q : 32 * q + 32 : 4, :],
            )

        picked0 = sb.tile([P, S], U32, name="picked0", tag="scales_then_words", align_bytes=256)
        nc.vector.tensor_copy(picked0[:], word_tables[0][:].bitcast(U32).indirect(offsets[:]))

        ident = sb.tile([P, P], F32, name="ident")
        make_identity(nc, ident[:])
        apo_dv = placed.tile([P, D, VH], F32, name="apo_dv", offset=0)
        apo_vd2 = placed.tile([P, VH, D], F32, name="apo_vd2", offset=2048)
        for g in range(2):
            apo_ps = ps.tile([P, 4, V], F32, name=f"apo_ps{g}", tag=f"spread{g}")
            for i in range(4):
                d = 4 * g + i
                nc.tensor.transpose(apo_ps[:, i, :], apo_vd[:, d : d + 1].to_broadcast([P, P]), ident[:])
            nc.scalar.copy(apo_dv[:, 4 * g : 4 * g + 4, :], apo_ps[:, :, :VH])
            nc.scalar.copy(apo_vd2[:, :, 4 * g : 4 * g + 4], apo_ps[:, :, VH:].rearrange("p d v -> p v d"))

        warm = ps.tile([P, M], F32, name="warm", tag="spread1")
        nc.tensor.matmul_mx(
            out=warm[:],
            lhsT=w_codes[:, :M].bitcast(FP8X4),
            lhsT_scale=w_plane[:, :M],
            rhs=w_codes[:, M:].bitcast(FP8X4),
            rhs_scale=w_plane[:, M:],
            start=True,
            stop=True,
        )

        widths = {0: QUARTER, 2 * EIGHTH: EIGHTH, 3 * EIGHTH: EIGHTH, HALF: QUARTER, 6 * EIGHTH: EIGHTH, 7 * EIGHTH: EIGHTH}
        y = {first: ps.tile([P, n], F32, name=f"y{first}", tag=f"y{first}") for first, n in widths.items()}
        picked1 = sb.tile([P, S], U32, name="picked1", align_bytes=64)

        def product(first, o, picked):
            cols = slice(first, first + widths[first])
            nc.tensor.matmul_mx(
                out=y[first][:],
                lhsT=w_codes[:, o * M : (o + 1) * M].bitcast(FP8X4),
                lhsT_scale=w_plane[:, o * M : (o + 1) * M],
                rhs=picked[:, cols].bitcast(FP8X4),
                rhs_scale=x_planes[:, o * S + first : o * S + first + widths[first]],
                start=(o == 0),
                stop=(o == PASSES - 1),
            )

        for c in range(4):
            nc.vector.tensor_copy(
                picked1[:, c * QUARTER : (c + 1) * QUARTER],
                word_tables[1][:].bitcast(U32).indirect(offsets[:, c * QUARTER // 16 : (c + 1) * QUARTER // 16]),
            )
            for o, picked in enumerate((picked0, picked1)):
                for first in widths:
                    if first // QUARTER == c:
                        product(first, o, picked)

        def foci(first):
            return slice(first // D, (first + widths[first]) // D)

        def foci2(first):
            return slice((first - HALF) // D, (first - HALF + widths[first]) // D)

        def y_dv(first):
            return y[first][:].rearrange("p (v d) -> p d v", d=D)

        def y_vd(first):
            return y[first][:].rearrange("p (v d) -> p v d", d=D)

        def add_transposed(bank, tiles):
            for i, tile in enumerate(tiles):
                nc.tensor.matmul(bank, tile, ident[:], start=(i == 0), stop=(i == len(tiles) - 1), is_transpose=True)

        def back_doubled(bank, pairs):
            nc.tensor.matmul(bank, pairs, ident[:], start=True, stop=False, is_transpose=True)
            nc.tensor.matmul(bank[:, ::-1, :], pairs, ident[:], start=False, stop=True, is_transpose=True)

        stacked = sb.tile([P, D, 2, VH], F32, name="stacked", tag="stacked_then_late")
        y_first = sb.tile([P, D, VH], F32, name="y_first")
        low, high = slice(0, D // 2), slice(D // 2, D)
        first_quarter, third_eighth, fourth_eighth = foci(0), foci(2 * EIGHTH), foci(3 * EIGHTH)

        def weigh_copy(ds, vs):
            nc.gpsimd.tensor_tensor(stacked[:, ds, 0, vs], y_first[:, ds, vs], apo_dv[:, ds, vs], ALU.mult)

        nc.scalar.copy(y_first[:, :, first_quarter], y_dv(0))
        nc.vector.tensor_tensor(stacked[:, :, 0, first_quarter], y_dv(0), apo_dv[:, :, first_quarter], ALU.mult)
        nc.scalar.copy(y_first[:, :, third_eighth], y_dv(2 * EIGHTH))
        nc.vector.tensor_tensor(stacked[:, :, 0, third_eighth], y_dv(2 * EIGHTH), apo_dv[:, :, third_eighth], ALU.mult)
        nc.scalar.activation(stacked[:, low, 1, first_quarter], y_first[:, low, first_quarter], ACT.Square, scale=sq_scale[:])
        nc.scalar.copy(y_first[:, :, fourth_eighth], y_dv(3 * EIGHTH))
        for ds in (low, high):
            weigh_copy(ds, fourth_eighth)
        nc.scalar.activation(stacked[:, high, 1, :VQ], y_first[:, high, :VQ], ACT.Square, scale=SQ_SCALE)
        nc.scalar.activation(stacked[:, low, 1, VQ:], y_first[:, low, VQ:], ACT.Square, scale=SQ_SCALE)

        held = placed.tile([P, 3 * QUARTER + VH], F32, name="held", offset=HELD)
        ys2 = held[:, :HALF].rearrange("p (v d) -> p v d", d=D)
        ys_third, ys_last = ys2[:, :VQ], ys2[:, VQ:]
        sq_last = held[:, HALF : 3 * QUARTER].rearrange("p (u v e) -> p u v e", u=2, e=D // 2)
        y_sum2 = held[:, 3 * QUARTER :]

        def square_last(i):
            nc.scalar.activation(
                sq_last[:, :, i * VE : (i + 1) * VE],
                y[(6 + i) * EIGHTH][:].rearrange("p (v u e) -> p u v e", u=2, e=D // 2),
                ACT.Square,
                scale=SQ_SCALE,
            )

        square_last(0)
        nc.scalar.activation(stacked[:, high, 1, VQ:], y_first[:, high, VQ:], ACT.Square, scale=SQ_SCALE)
        square_last(1)
        for first in (HALF, 6 * EIGHTH, 7 * EIGHTH):
            vs = foci2(first)
            nc.vector.tensor_tensor(ys2[:, vs], y_vd(first), apo_vd2[:, vs, :], ALU.mult)
            nc.vector.tensor_reduce(y_sum2[:, vs], y_vd(first), AX.X, ALU.add)

        sq_third = sb.tile([P, VQ, D], F32, name="sq_third")
        nc.scalar.activation(sq_third[:].rearrange("p v d -> p (v d)"), y[HALF][:], ACT.Square, scale=SQ_SCALE)
        y_pairs_t = ps.tile([P, M], F32, name="y_pairs_t", tag="spread0")
        add_transposed(y_pairs_t[:], [y_first[:, 2 * i : 2 * i + 2].rearrange("p e v -> p (e v)") for i in range(D // 2)])
        y_pairs = sb.tile([P, M], F32, name="y_pairs", tag="pairs_then_abs")
        nc.scalar.copy(y_pairs[:], y_pairs_t[:])
        ys_pairs = sb.tile([P, VQ, D // 2], F32, name="ys_pairs", tag="pairs_then_energy")
        nc.gpsimd.tensor_tensor(ys_pairs[:], ys_third[:, :, low], ys_third[:, :, high], ALU.add)
        sq_pairs = sb.tile([P, VQ, D // 2], F32, name="sq_pairs")
        nc.gpsimd.tensor_tensor(sq_pairs[:], sq_last[:, 0], sq_last[:, 1], ALU.add)
        beam2 = sb.tile([P, VH], F32, name="beam2", tag="beam_then_ln")
        nc.vector.tensor_reduce(beam2[:, :VQ], ys_pairs[:], AX.X, ALU.add)
        nc.vector.tensor_reduce(beam2[:, VQ:], ys_last, AX.X, ALU.add)
        energy2 = sb.tile([P, VH], F32, name="energy2", tag="pairs_then_energy")
        nc.vector.tensor_reduce(energy2[:, :VQ], sq_third[:], AX.X, ALU.add)
        nc.vector.tensor_reduce(energy2[:, VQ:], sq_pairs[:], AX.X, ALU.add)

        sums_t = ps.tile([P, M], F32, name="sums_t", tag="spread1")
        add_transposed(sums_t[:], [stacked[:, d].rearrange("p s v -> p (s v)") for d in range(D)])
        abs_t = sb.tile([P, M], F32, name="abs_t")
        nc.scalar.activation(abs_t[:], sums_t[:], ACT.Abs)

        y_sum1 = ps.tile([P, 2, VH], F32, name="y_sum1", tag="y0")
        back_doubled(y_sum1[:], y_pairs[:])
        sums1 = ps.tile([P, 2, VH], F32, name="sums1", tag=f"y{2 * EIGHTH}")
        nc.tensor.transpose(sums1[:].rearrange("p s v -> p (s v)"), abs_t[:], ident[:])
        sums1_again = ps.tile([P, 2, VH], F32, name="sums1_again", tag=f"y{3 * EIGHTH}")
        nc.tensor.transpose(sums1_again[:].rearrange("p s v -> p (s v)"), abs_t[:], ident[:])

        late = sb.tile([P, V], F32, name="late", tag="stacked_then_late")
        ln_den1, sum_sq2 = late[:, :VH], late[:, VH:]
        beam2_abs = sb.tile([P, VH], F32, name="beam2_abs", tag="pairs_then_abs")
        sum_sq1 = sb.tile([P, VH], F32, name="sum_sq1")
        nc.scalar.activation(sum_sq2, y_sum2, ACT.Square)
        nc.scalar.activation(sum_sq1[:], y_sum1[:, 0, :], ACT.Square)
        nc.scalar.activation(beam2_abs[:], beam2[:], ACT.Abs)
        ln_den2 = sb.tile([P, VH], F32, name="ln_den2", tag="beam_then_ln")
        nc.scalar.activation(ln_den2[:], energy2[:], ACT.Ln, bias=0.1 * LN_SHIFT, scale=20.0 * LN_SHIFT)
        nc.scalar.activation(ln_den1, sums1_again[:, 1, :], ACT.Ln, bias=0.1 * LN_SHIFT, scale=20.0 * LN_SHIFT)

        power = sb.tile([P, V], F32, name="power")
        num = sb.tile([P, V], F32, name="num")
        nc.vector.tensor_tensor(power[:, :VH], sums1[:, 0, :], sum_sq1[:], ALU.mult)
        nc.vector.tensor_tensor(power[:, VH:], beam2_abs[:], sum_sq2, ALU.mult)
        nc.vector.tensor_tensor(num[:, :VH], sums1[:, 1, :], power[:, :VH], ALU.add)
        nc.vector.tensor_tensor(num[:, VH:], energy2[:], power[:, VH:], ALU.add)
        ln_num = sb.tile([P, V], F32, name="ln_num")
        result = sb.tile([P, V], F32, name="result")
        for vs, ln_den in ((slice(0, VH), ln_den1), (slice(VH, V), ln_den2[:])):
            nc.scalar.activation(ln_num[:, vs], num[:, vs], ACT.Ln, bias=0.005 * LN_SHIFT, scale=LN_SHIFT)
            nc.vector.tensor_tensor(result[:, vs], ln_num[:, vs], ln_den, ALU.subtract)
        nc.sync.dma_start(out, result[:])
